import numpy as np, ml_dtypes
CORES = [16,17,18,19,32,33,34,35]
N = 8
BF = ml_dtypes.bfloat16
def gentries(a):
    return np.ascontiguousarray(a.reshape(8, 16, -1).transpose(0, 2, 1)).reshape(8, -1)
def gtable(e):
    e = np.asarray(e); return np.ascontiguousarray(e.reshape(8, -1, 16).transpose(0, 2, 1)).reshape(128, -1).astype(np.int32)
def f(rng, *shape):
    return (rng.standard_normal(shape, dtype=np.float32) * np.exp2(rng.integers(-2, 3, shape[:-1] + (1,)))).astype(BF)
def wide(rng, *shape):
    v = f(rng, *shape).astype(np.float32); k = shape[:-2] + (1, shape[-1])
    return (v * np.exp2(rng.integers(-6, 7, k)) * (rng.random(k) > 0.0625)).astype(BF)
V, G, S, P, RO, VO = 1280, 384, 384, 4, 4, 10
def parts(rng):
    sd = (rng.random((N, 8, V)) < 0.3 + 0.4 * rng.random((N, 8, 1))).astype(np.int64)
    nr = rng.integers(0, S, (N, 8, V)); hs = np.ascontiguousarray(np.argsort(rng.random((N, 8, V)), axis=-1)[..., :S])
    tl = rng.integers(0, V, (N, 8, 16, V)); tl = np.where(rng.random(tl.shape) < 0.2, V + rng.integers(0, G, tl.shape), tl)
    u = 0.6 * rng.standard_normal((N, 8, 16, V)) + np.where(sd == 0, 0.5, -0.5)[:, :, None, :]
    c = 0.5 * rng.standard_normal((N, 8, 16, S)); lean = 0.4 * rng.choice(np.array([-1.0, -0.5, 0.0, 0.5, 1.0]), (N, 8, 1, S))
    w = np.stack([c + lean + 0.3 * rng.standard_normal(c.shape), c - lean + 0.3 * rng.standard_normal(c.shape)], axis=-1)
    th = rng.integers(0, 48, (N, 8, 16, 1)) * 0.015625
    return sd, nr, hs, tl, u, w, th
def pack(sd, nr, hs, tl, u, w, th):
    def cut(a, n): return np.where(np.abs(a) < 2.0 ** -20, 0.0, np.clip(a, -2.0, 2.0)).reshape(N, 128, n).astype(np.float32).astype(BF)
    return {"tl": np.ascontiguousarray(tl.reshape(N, 128, V)).astype(np.int32), "u0": cut(u, V), "w0": cut(w, 2 * S), "sd": sd.astype(np.int32), "nr": nr.astype(np.int32),
            "hs": hs.astype(np.int32), "th": th.reshape(N, 128, 1).astype(np.float32)}
def still(rng, p, r, g, up, fine):
    sd, nr, hs, tl, u, w, th = p
    a1 = rng.integers(-48, 49, (16, 1)) * 0.015625; gap = rng.integers(1, 65, (16, 1)) * 0.015625; sign = 1.0 if up else -1.0; a0 = a1 + sign * gap
    tl[r, g] = tl[r, g] % V; u[r, g] = np.where(sd[r, g] == 0, a0, a1)
    n = rng.choice(np.array([0, 1, VO - 1, VO - 1, VO, VO, 15, 16]), S); m = np.argsort(rng.random((16, S)), axis=0) < n
    w[r, g, :, :, 0] = a0 + sign * np.where(m, 0.0078125, 0.0); w[r, g, :, :, 1] = a1
    th[r, g] = gap + (0.0078125 - 0.000244140625 if fine else 0.0)
def hang(rng, p, r, g, up):
    sd, nr, hs, tl, u, w, th = p; z = 0 if up else 1
    kind = rng.permutation(np.arange(16) % 3)[:, None]; m = 1 + rng.integers(1, 64, (16, 1)) * 0.0078125; j = rng.integers(1, 17, (16, 1)) * 0.0078125
    base = np.where(kind == 0, -2.0 ** -20 - 2.0 ** -27, np.where(kind == 1, m, (2 * rng.integers(64, 128, (16, 1)) + 1) * 2.0 ** -17))
    at = np.where(kind == 1, m + j, m); dif = (at - base).astype(np.float32)
    th[r, g] = np.where(kind == 0, dif, np.nextafter(dif, np.float32(0)))
    o = np.argsort(rng.random((16, S)), axis=0); step = rng.integers(1, 33, (16, S)) * 0.0078125
    w[r, g, :, :, z] = at + np.where(o < VO - 1, step, np.where(o == VO - 1, 0.0, -step)); w[r, g, :, :, 1 - z] = base
    sd[r, g] = 1 - z; tl[r, g] = tl[r, g] % V; u[r, g] = base
def full(rng, p, r, g, c):
    sd, nr, hs, tl, u, w, th = p; E = S // 2; z = int(rng.integers(0, 2))
    v = np.arange(V)
    if c in (1, 3, 6): v = np.roll(v, E - G)
    if c in (4, 7): v = rng.permutation(V)
    to = np.zeros(S, np.int64); to[0::2] = rng.permutation(v[:E]); to[1::2] = rng.permutation(v[E:S]); sd[r, g, to] = 1 - z
    if c < 2: to[S - 2] = to[0]
    k = np.arange(16)[:, None]; k0 = rng.integers(0, 4, S); own = rng.integers(0, V, (16, S)); gh = V + rng.integers(0, G, (16, S))
    nm = np.where(k < k0, gh, np.where(k == k0, to, own))
    if c in (2, 3, 4): nm[:, 1::2] = gh[:, 1::2]
    tl[r, g][:, hs[r, g]] = nm
    h = 1.25 if z == 0 else -1.25
    u[r, g] = np.where(sd[r, g] == 0, h, -h) + 0.25 * (2 * rng.random((16, V)) - 1)
    w[r, g] = np.array([h, -h]) + 0.25 * (2 * rng.random((16, S, 2)) - 1)
    th[r, g] = rng.integers(0, 33, (16, 1)) * 0.015625
def setup_inputs(rng):
    return pack(*parts(rng))
def setup_inputs_spread(rng):
    sd, nr, hs, tl, u, w, th = parts(rng)
    u = wide(rng, N, 128, V).astype(np.float64).reshape(N, 8, 16, V) * 0.0625
    w = wide(rng, N, 128, 2 * S).astype(np.float64).reshape(N, 8, 16, S, 2) * 0.0625
    b = rng.integers(0, 3, (N, 8, 1, S, 1)); z = np.array([1.0, -1.0])
    w = np.where(b == 0, w, np.where(b == 1, np.abs(w) * z, -np.abs(w) * z))
    th = np.exp2(rng.integers(-10, 2, (N, 8, 16, 1))) * (rng.random((N, 8, 16, 1)) > 0.125)
    return pack(sd, nr, hs, tl, u, w, th)
def setup_inputs_ends(rng):
    sd, nr, hs, tl, u, w, th = parts(rng)
    def ends(shape, hi, share): return np.where(rng.random(shape) < share, hi * rng.integers(0, 2, shape), rng.integers(0, hi + 1, shape))
    nr = ends((N, 8, V), S - 1, 0.75); hs = ends((N, 8, S), V - 1, 0.75); tl = ends((N, 8, 16, V), V + G - 1, 0.75)
    u = np.where(rng.random((N, 8, 1, V)) < 0.5, 4.0 * rng.integers(0, 2, (N, 8, 1, V)) - 2, 4.0 * rng.integers(0, 2, (N, 8, 16, V)) - 2)
    z = np.array([2.0, -2.0]); b = rng.integers(0, 4, (N, 8, 1, S, 1)); free = 4.0 * rng.integers(0, 2, (N, 8, 16, S, 2)) - 2
    n = VO - rng.integers(0, 2, (N, 8, 1, S)); m = (np.argsort(rng.random((N, 8, 16, S)), axis=2) < n)[..., None]
    w = np.where(b == 0, z, np.where(b == 1, -z, np.where(b == 2, free, np.where(m, z, -2.0))))
    th = 2.0 * rng.integers(0, 2, (N, 8, 16, 1))
    tl = np.where(tl == G - 1, G - 2, np.where(tl == V - 1, V - 2, tl)); hs = np.where(hs == G - 1, G - 2, hs)
    for g in range(8):
        far = 2.0 if g % 2 == 0 else -2.0
        sd[:, g, G - 1] = 0; u[:, g, :, G - 1] = far; tl[:, g, :, G - 1] = G - 1
        if g in (0, 7):
            for v in (0, V - 1): sd[:, g, v] = 0; u[:, g, :, v] = far; tl[:, g, :, v] = V + G - 1
    return pack(sd, nr, hs, tl, u, w, th)
def setup_inputs_corners(rng):
    p = parts(rng); sd, nr, hs, tl, u, w, th = p
    for r in range(N):
        o = rng.permutation(8)
        for g in range(8):
            c = int(o[g])
            if c < 2: sd[r, g] = c
            elif c == 2: tl[r, g] = V + tl[r, g] % G
            elif c == 3: tl[r, g] = np.arange(V)
            elif c == 4:
                tl[r, g] = rng.choice(np.array([0, V - 1, V, V + G - 1]), (16, V)); hs[r, g] = np.where(rng.random(S) < 0.5, rng.choice(np.array([0, V - 1]), S), hs[r, g])
            elif c == 5:
                hs[r, g, 0::2] = int(rng.integers(0, V)); hs[r, g, 1::4] = V - 1; hs[r, g, 3::4] = 0; nr[r, g] = rng.choice(np.array([0, S - 1]), V)
            elif c == 6:
                own = rng.integers(0, V, (16, V)); gh = V + rng.integers(0, G, (16, V)); k = np.arange(16)[:, None]; v = np.arange(V)
                tl[r, g] = np.where(k == np.where(v % 2 == 0, 15, 0), own, gh)
            else: still(rng, p, r, g, r % 2 == 0, False)
    return pack(*p)
def setup_inputs_crowd(rng):
    p = parts(rng); sd, nr, hs, tl, u, w, th = p; most = rng.permutation(N)[:N // 2]
    for r in range(N):
        o = rng.permutation(8)
        for g in range(8):
            c = int(o[g])
            if r in most:
                full(rng, p, r, g, c); continue
            if c > 3: continue
            z = int(rng.integers(0, 2)); q = 1 + rng.permutation(V - 2)[:16]
            if c == 0: q[0] = V - 1
            if c == 1: q[0] = 0
            sd[r, g, q] = 1 - z; tl[r, g] = q[:, None]
            if c == 1:
                for j in (0, 1): tl[r, g, :, hs[r, g, 2 * int(rng.integers(0, S // 2)) + j]] = rng.integers(0, V, 16)
            if c == 2: tl[r, g] = q[(np.arange(16)[:, None] + np.arange(V) % 3) % 16]
            if c == 3: tl[r, g] = np.where(rng.random(V) < 0.5, rng.integers(0, V, (16, V)), tl[r, g])
            h = 1.25 if z == 0 else -1.25
            u[r, g] = np.where(sd[r, g] == 0, h, -h) + 0.25 * (2 * rng.random((16, V)) - 1)
            w[r, g] = np.array([h, -h]) + 0.25 * (2 * rng.random((16, S, 2)) - 1)
            th[r, g] = rng.integers(0, 33, (16, 1)) * 0.015625
    return pack(*p)
def setup_inputs_calm(rng):
    p = parts(rng)
    for r in range(N):
        o = rng.permutation(8)
        for g in range(8):
            c = int(o[g])
            if c < 4: still(rng, p, r, g, c % 2 == 0, c > 1)
            elif c < 6: hang(rng, p, r, g, c == 4)
    return pack(*p)
def check_inputs(d):
    bad = []
    for k, lo, hi in (("tl", 0, V + G - 1), ("u0", -2, 2), ("w0", -2, 2), ("sd", 0, 1), ("nr", 0, S - 1), ("hs", 0, V - 1), ("th", 0, 2)):
        a = np.asarray(d[k]).astype(np.float64)
        if not (np.min(a) >= lo and np.max(a) <= hi): bad.append("range of " + k)
        if k in ("u0", "w0", "th") and np.any((a != 0) & (np.abs(a) < 2.0 ** -20)): bad.append("least size of " + k)
    return bad
def tree(q):
    for h in (8, 4, 2, 1): q = q[..., :h, :] + q[..., h:, :]
    return q[..., 0, :]
def ext(a):
    b = np.roll(a, -1, axis=0)
    return np.concatenate([a, b[..., :G // 2], np.roll(b, -1, axis=1)[..., G // 2:G]], axis=-1)
def reference(tl, u0, w0, sd, nr, hs, th):
    t = tl.astype(np.int64).reshape(N, 8, 16, V); u = np.array(u0.astype(np.float32).reshape(N, 8, 16, V)); w = np.array(w0.astype(np.float32).reshape(N, 8, 16, S, 2))
    side = sd.astype(np.int64); near = nr.astype(np.int64); host = hs.astype(np.int64); lim = th.astype(np.float32).reshape(N, 8, 16, 1); c = np.float32(0.015625)
    for rnd in range(RO):
        view = [ext(np.where((side == z)[:, :, None, :], u, np.take_along_axis(w[..., z], near[:, :, None, :], 3))) for z in (0, 1)]
        es = ext(side)
        v = np.arange(rnd % P, V, P); ix = t[..., v] + (V + G) * side[..., v][:, :, None, :]
        x = np.take_along_axis(np.concatenate(view, axis=3), ix.reshape(N, 8, 1, -1), 3).reshape(N, 8, 16, 16, len(v))
        d = x - u[..., v][..., None, :]; nu = u.copy(); nu[..., v] = u[..., v] + tree(d * np.abs(d)) * c
        s = np.arange(rnd % 2, S, 2); name = np.take_along_axis(t, host[..., s][:, :, None, :], 3)
        flat = name.reshape(N, 8, -1); e = np.take_along_axis(es, flat, 2).reshape(name.shape)
        x = np.take_along_axis(np.where((es == 0)[:, :, None, :], view[0], view[1]), flat[:, :, None, :], 3).reshape(N, 8, 16, 16, len(s))
        new = []
        for z in (0, 1):
            old = w[..., z][..., s]; d = np.where((e == z)[:, :, None], x - old[..., None, :], np.float32(0))
            new.append(old + tree(d * np.abs(d)) * c)
        diff = new[0] - new[1]
        up = np.count_nonzero(diff > lim, axis=2) >= VO; dn = np.count_nonzero(diff < -lim, axis=2) >= VO
        sg = np.where(up, 0, 1); fit = (up | dn)[:, :, None] & (name < V) & (e == 1 - sg[:, :, None])
        k = np.argmax(fit, axis=2); ok = np.any(fit, axis=2)
        claim = np.where(ok, np.take_along_axis(name, k[:, :, None], 2)[:, :, 0], V)
        a, b, i = np.nonzero(ok); first = np.full((N, 8, V + 1), S, np.int64); np.minimum.at(first, (a, b, claim[a, b, i]), i)
        a, b, i = np.nonzero(ok & (np.take_along_axis(first, claim, 2) == np.arange(len(s))))
        n = claim[a, b, i]; z = sg[a, b, i]
        w[..., s, 0] = new[0]; w[..., s, 1] = new[1]; u = nu
        u[a, b, :, n] = w[a, b, :, s[i], z]; side[a, b, n] = z; near[a, b, n] = s[i]; host[a, b, s[i]] = n
    return {"yu": u.reshape(N, 128, V), "ys": w.reshape(N, 128, 2 * S), "yc": (2 * near + side).astype(np.float32), "yh": host.astype(np.float32)}

@@ -1,0 +1,680 @@
+import math
+from concourse.bass import DstId, RemoteDMATransfer
+from concourse.mybir import AluOpType, ActivationFunctionType
+
+CFG = {"A": ["s0", "s1", "s2"], "lastA": ["s0", "s1", "s2"],
+       "pes": (0,), "pea": False, "l3": (), "wf": (0,), "ss": True, "us": True, "sv": False, "ev": (1,),
+       "psub": (0, 2, 4), "xg": {}, "vv": ("g", "n4"), "fb": 3, "ls": 1200, "seed": 0, "noise": 0.0}
+RO = 4
+F, B, I, U = "float32", "bfloat16", "int32", "uint16"
+BUF = {
+    "UW": (2240, F), "C": (1472, F), "TL": (1280, I), "IN": (1280, I), "XG": (3072, F), "TH": (8, F),
+    "D0": (1024, F), "D1": (1024, F), "D2": (1024, F), "WS0": (1024, F), "WS1": (1024, F), "WS2": (1024, F),
+    "DA0": (1024, F), "DA1": (1024, F), "QS0": (1024, F), "QS1": (1024, F), "QW0": (2048, F), "QW1": (2048, F), "QW2": (2048, F), "R32": (128, F),
+    "PM": (512, F), "PB": (512, B), "PK": (512, B), "KW": (192, F),
+    "EB": (3072, B), "EL": (192, B), "IX": (576, U), "NM0": (192, F), "NM1": (192, F), "NU0": (192, U), "NU1": (192, U),
+    "SG0": (192, B), "SG1": (192, B), "FIT": (384, B), "VAL": (384, F), "CAND": (384, F),
+    "TI": (320, U), "TF": (1280, F), "UC": (320, F), "UB": (320, B), "MK": (192, F), "HL": (24, F), "HU": (24, U), "HA": (24, F), "YH": (256, F),
+    "DD": (192, F), "CMP": (384, B), "MM": (384, F), "VV": (192, F), "PR": (192, F), "S1": (192, F), "S2": (192, F),
+    "EQ": (1248, B), "PU": (12, U), "MW": (384, F), "DN": (384, F),
+    "CI": (160, I), "VA": (160, F), "VL": (160, U), "ST": (384, B), "SV": (384, F),
+    "IK": (128, B), "JF": (192, F), "JG": (128, F), "PI": (8, I), "PF": (16, F), "OH": (16, F), "T1": (192, F), "T2": (192, F), "TJ": (192, F),
+    "I32": (128, F), "IB": (128, B), "IH": (128, B), "IN1": (128, B), "ROT": (128, B),
+    "BO32": (128, F), "BOB": (128, B), "BOK": (128, B), "MT": (128, B), "WA": (512, B), "RR": (384, F),
+    "D32": (2048, F), "DB": (2048, B), "DG": (192, F), "KEEP": (192, F), "TD": (192, F), "THR": (192, F), "WT": (192, F),
+    "W2S": (384, F), "KA": (96, F), "ML": (160, F),
+}
+for _t in range(RO):
+    BUF["X%d" % _t] = (3328, F)
+    BUF["SD%d" % _t] = (1856, B)
+PS = {"P0": 1024, "P1": 1024, "P2": 1024, "M0": 512, "M1": 512}
+ALIAS = {"RR": "MW", "VAL": "MM", "JG": "VV", "TJ": "DN", "T1": "MK", "T2": "UC"}
+SCRATCH = {k: ("sbuf", [128, v[0]], v[1]) for k, v in BUF.items() if k not in ALIAS}
+for _k, _v in PS.items():
+    SCRATCH[_k] = ("psum", [128, _v], F)
+
+
+def A(name, lo=0, n=None, step=1, p=(0, 128)):
+    if n is None:
+        n = (BUF[name][0] if name in BUF else PS[name]) - lo
+    return {"b": ALIAS.get(name, name), "lo": lo, "n": n, "st": step, "p": p}
+
+
+def IND(win, off):
+    return {"b": win["b"], "lo": win["lo"], "n": 16 * off["n"], "st": 1, "p": (0, 128), "wn": win["n"], "off": off}
+
+
+def isap(x):
+    return isinstance(x, dict)
+
+
+def span(a):
+    return (a["b"], a["lo"], a["lo"] + (a["wn"] if "off" in a else (a["n"] - 1) * a["st"] + 1), a["st"], a["p"])
+
+
+def meet(a, b):
+    if a[1] >= b[2] or b[1] >= a[2] or a[4][0] >= b[4][1] or b[4][0] >= a[4][1]: return False
+    return (a[1] - b[1]) % math.gcd(a[3], b[3]) == 0
+
+
+def build_ops(cfg):
+    ops = []
+
+    def add(e, kind, outs, ins, cost, **kw):
+        rd, wr = [], []
+        for a in outs:
+            wr.append(span(a))
+            if "off" in a: rd.append(span(a["off"]))
+        for a in ins:
+            if isap(a):
+                rd.append(span(a))
+                if "off" in a: rd.append(span(a["off"]))
+        d = {"e": e, "k": kind, "rd": rd, "wr": wr, "cost": cost, "lat": 0.0}
+        d.update(kw)
+        ops.append(d)
+        return len(ops) - 1
+
+    def vc(out, i0, c):
+        n = out["n"]
+        if "off" in out: return 0.05 + n * 3.8 * 0.00083
+        if "off" in i0: return 0.05 + n * 1.56 * 0.00083
+        return 0.02 + max(64, n * c) * 0.00083
+
+    def two(*a):
+        return all(x["b"] in BUF and BUF[x["b"]][1] in (B, U) for x in a)
+
+    def tt(o, a, b, op):
+        c = 1 if (a["b"] in PS or b["b"] in PS) else 2
+        return add("V", "tt", [o], [a, b], vc(o, a, c), a=(o, a, b, op))
+
+    def ts(o, a, s1, op0, s2=None, op1=None):
+        return add("V", "ts", [o], [a, s1, s2], vc(o, a, 0.5 if two(o, a) else 1), a=(o, a, s1, s2, op0, op1))
+
+    def cp(o, a):
+        return add("V", "cp", [o], [a], vc(o, a, 0.5 if two(o, a) else 1), a=(o, a))
+
+    def ms(o, v):
+        return add("V", "ms", [o], [], vc(o, o, 1), a=(o, v))
+
+    def scan(o, d0, d1, init, op0, op1):
+        return add("V", "scan", [o], [d0, d1], vc(o, d0, 1), a=(o, d0, d1, init, op0, op1))
+
+    def act(o, a, f, bias=0.0, scale=1.0):
+        return add("S", "act", [o], [a, bias, scale], vc(o, a, 1) + 0.02, a=(o, a, f, bias, scale))
+
+    def mm(o, l, r, start=True, stop=True):
+        w = 4 if BUF[r["b"]][1] == F else 1
+        return add("T", "mm", [o], [l, r] + ([] if start else [o]), 0.01 + max(64, r["n"]) * w * 0.00042, a=(o, l, r, start, stop), acc=not start)
+
+    def iota(o, pat, base, cm):
+        return add("G", "iota", [o], [], 0.13 + o["n"] * 2 * 0.00083, a=(o, pat, base, cm))
+
+    def dma(q, o, a, nbytes):
+        return add(q, "dma", [o] if isap(o) else [], [a], 1.0 if q == "G" else 0.1, a=(o, a), lat=1.9 + nbytes / 2e5)
+
+    def col(name, c):
+        return A(name, c, 1)
+
+    ALL = (slice(None), slice(None))
+    dma("Y", A("IN", 0, 1280, p=(0, 8)), ("sd", ALL), 4e4)
+    dma("Y", A("IN", 0, 1280, p=(8, 16)), ("nr", ALL), 4e4)
+    dma("Y", A("IN", 0, 384, p=(16, 24)), ("hs", ALL), 1e4)
+    dma("S", A("EB", 1280, 768), ("w0", ALL), 2e5)
+    dma("S", A("EB", 0, 1280), ("u0", ALL), 3.3e5)
+    dma("Y", A("TL"), ("tl", ALL), 6.6e5)
+    dma("Y", col("TH", 4), ("th", ALL), 1e3)
+    iota(col("PI", 0), [[0, 1]], 0, 1)
+    iota(A("JF"), [[1, 192]], 0, 0)
+    iota(A("JG"), [[1, 8], [0, 16]], 0, 0)
+    iota(A("TJ"), [[0, 12], [1, 16]], 0, 0)
+    iota(A("W2S"), [[2, 384]], 0, 0)
+    cp(col("PF", 0), col("PI", 0))
+    for c, (s, op) in enumerate(((15, "and"), (4, "shr"), (7, "and"), (3, "shr"))):
+        ts(col("PI", 1 + c), col("PI", 0), s, op)
+    cp(A("PF", 1, 4), A("PI", 1, 4))
+    ts(col("PF", 4), col("PF", 4), 1.0, "add")
+    ts(col("PF", 5), col("PF", 0), 16.0, "ge")
+    ts(A("RR", 0, 128), A("JG"), col("PF", 3), "eq", col("PF", 4), "mul")
+    ts(A("RR", 128, 128), A("JG"), col("PF", 3), "eq", 1664.0, "mul")
+    ts(A("RR", 256, 128), A("JG"), col("PF", 3), "eq", col("PF", 5), "mul")
+    ts(A("I32"), A("JF", 0, 128), col("PF", 0), "eq")
+    ts(A("OH"), A("JF", 0, 16), col("PF", 1), "eq")
+    for b in range(16):
+        act(A("D32", 128 * b, 128), A("I32"), "Copy", 0.0, col("OH", b))
+    act(A("IB"), A("I32"), "Copy")
+    act(A("R32", 0, 112), A("I32", 16, 112), "Copy")
+    act(A("R32", 112, 16), A("I32", 0, 16), "Copy")
+    act(A("ROT"), A("R32"), "Copy")
+    for z in (0, 1):
+        ts(A("ML", 80 * z, 80), A("JF", 0, 80), 16.0, "mul", col("PF", 1), "add")
+    ts(A("DG"), A("TJ"), col("PF", 1), "eq")
+    act(A("KEEP"), A("TJ"), "Sign")
+    dma("G", A("DB"), A("D32"), 5e5)
+    act(A("IH"), A("I32"), "Copy", 0.0, 0.5)
+    act(A("IN1"), A("I32"), "Copy", 0.0, -1.0)
+    act(A("IK"), A("I32"), "Copy", 0.0, 2048.0)
+    ts(A("BO32"), A("JG"), col("PF", 2), "eq")
+    act(A("BOB"), A("BO32"), "Copy")
+    act(A("BOK"), A("BO32"), "Copy", 0.0, 8192.0)
+    ts(A("T1", 0, 128), A("JF", 0, 128), col("PF", 0), "gt", -2048.0, "mul")
+    tt(A("MT"), A("T1", 0, 128), A("BO32"), "mul")
+    ts(col("TH", 1), col("TH", 4), -1.0, "mul")
+    ts(col("PF", 7), col("PF", 1), 8.0, "ge", 512.0, "mul")
+    ts(col("PF", 7), col("PF", 7), 512.0, "add")
+    ts(col("PI", 5), col("PI", 0), 3, "and")
+    ts(col("PI", 6), col("PI", 0), 2, "shr", 1, "and")
+    ts(col("PI", 7), col("PI", 0), 3, "shr", 1, "and")
+    cp(A("PF", 8, 3), A("PI", 5, 3))
+    ts(col("PF", 11), col("PF", 10), -1.0, "mul", 1.0, "add")
+    ts(col("PF", 12), col("PF", 10), -8.0, "mul", col("PF", 0), "add")
+    ts(col("PF", 13), col("PF", 10), 4.0, "mul")
+    ts(A("S1", 0, 144), A("JF", 0, 144), -16.0, "add", col("PF", 12), "eq")
+    ts(col("PF", 15), col("PF", 2), 16.0, "mul", col("PF", 8), "add")
+    ts(A("S2", 0, 144), A("JF", 0, 144), -16.0, "add", col("PF", 15), "eq")
+    tt(A("PR", 4, 140), A("S2", 0, 140), A("S2", 4, 140), "sub")
+    tt(col("PF", 6), col("PF", 7), col("PF", 9), "mul")
+    tt(col("PF", 7), col("PF", 7), col("PF", 6), "sub")
+    for hf in (0, 1):
+        for sg in (0, 1):
+            act(A("PM", 128 * (2 * hf + sg), 128), A("S1", 16 - 8 * sg, 128), "Copy", 0.0, col("PF", 11 - hf))
+            act(A("WA", 128 * (2 * hf + sg), 128), A("PR", 16 - 8 * sg, 128), "Copy", 0.0, col("PF", 7 - hf))
+    act(A("PB"), A("PM"), "Copy")
+    act(A("PK"), A("PM"), "Copy", 0.0, 1664.0)
+    ts(A("KW", 0, 96), A("JF", 0, 96), 8.0, "mul", col("PF", 13), "add")
+    ts(A("KW", 96, 96), A("KW", 0, 96), 2.0, "add")
+    ts(col("PF", 9), col("PF", 9), -1536.0, "mul", 1536.0, "add")
+    ts(col("PF", 14), col("PF", 10), 8.0, "mul", col("PF", 8), "add")
+    tt(col("PF", 14), col("PF", 14), col("PF", 9), "add")
+    ts(A("KA", 0, 48), A("JF", 0, 48), 16.0, "mul", col("PF", 14), "add")
+    ts(A("KA", 48, 48), A("KA", 0, 48), 4.0, "add")
+    ms(A("T1"), 0.5)
+    iota(A("T2"), [[0, 192]], 0, 0)
+    scan(A("PR"), A("T1"), A("T2"), 2.0 ** 97, "mul", "add")
+    tt(A("THR"), A("PR"), A("DG"), "mul")
+    scan(A("PR"), A("KEEP"), A("THR"), 0.0, "mul", "add")
+    act(A("WT"), A("PR"), "Copy", 0.0, 0.5)
+    iota(A("DD"), [[-1, 192]], 191, 0)
+    ts(A("T2"), A("KEEP"), 1e6, "mul", col("PF", 1), "sub")
+    tt(A("TD"), A("DD"), A("T2"), "add")
+    for b in range(3):
+        iota(A("QW%d" % b, 0, 512), [[0, 512]], 0, 0)
+    for b in ("UW", "C", "SD1", "SD2", "SD3"):
+        iota(A(b, 0, 192), [[0, 192]], 0, 0)
+    cp(A("XG", 0, 384, p=(0, 24)), A("IN", 0, 384, p=(0, 24)))
+    cp(A("XG", 384, 896, p=(0, 16)), A("IN", 384, 896, p=(0, 16)))
+    cp(A("TF", 0, 640), A("TL", 0, 640))
+    cp(A("TF", 640, 640), A("TL", 640, 640))
+    act(A("UW", 1472, 768), A("EB", 1280, 768), "Copy")
+    act(A("UW", 192, 384), A("EB", 0, 384), "Copy")
+    act(A("UW", 576, 896), A("EB", 384, 896), "Copy")
+    for k, (lo, n) in enumerate(((0, 384), (384, 512), (896, 384))):
+        mm(A("P%d" % k, 0, n), A("RR", 0, 128, p=(0, 16)), A("XG", lo, n, p=(0, 16)))
+        cp(A("C", 192 + lo, n), A("P%d" % k, 0, n))
+        mm(A("P%d" % k, 512, n), A("RR", 128, 128, p=(0, 8)), A("XG", lo, n, p=(0, 8)))
+        act(A("SD0", 192 + lo, n), A("P%d" % k, 512, n), "Copy")
+
+    def send_sides(t):
+        sd = "SD%d" % t
+        mm(A("M0", 0, 192), A("IB"), A(sd, 192, 192))
+        mm(A("M0", 192, 192), A("ROT"), A(sd, 384, 192))
+        act(A("ST"), A("M0", 0, 384), "Copy")
+        s = add("G", "rem", [], [A("ST")], 1.0, tr=[(A(sd, 1472, 384), A("ST"))], sem="as%d" % t, lat=1.5)
+        add("R", "arr", [A(sd, 1472, 384)], [], 0.0, sem="as%d" % t, ntr=1, after=s, lat=1.0)
+
+    def view_lists(c0, c1):
+        n = c1 - c0
+        for b in range(16):
+            mm(A("M1", 384 + c0, n), A("D32", 128 * b, 128), A("C", 192 + 16 * c0 + b, n, 16), b == 0, b == 15)
+        cl = A("M1", 384 + c0, n)
+        cp(A("CI", c0, n), cl)
+        ts(A("CI", 80 + c0, n), A("CI", c0, n), 1, "and")
+        for z in (0, 1):
+            v = A("VA", 80 * z + c0, n)
+            ts(v, A("CI", 80 + c0, n), (4096.0, -4096.0)[z], "mul", (1279.0 - 4096.0, 1281.0)[z], "add")
+            tt(v, v, cl, "add")
+        for lo, m in (((0, 160),) if n == 80 else ((c0, n), (80 + c0, n))):
+            tt(A("VA", lo, m), A("VA", lo, m), A("ML", lo, m), "max")
+            cp(A("VL", lo, m), A("VA", lo, m))
+
+    def views(t, c0, c1, split=False):
+        for z in (0, 1):
+            o, a = A("X%d" % t, 1664 * z + 16 * c0, 16 * (c1 - c0)), IND(A("UW", 192, 2048), A("VL", 80 * z + c0, c1 - c0))
+            if split and z: cp(o, a)
+            else: act(o, a, "Copy")
+
+    def send_views(t):
+        x = "X%d" % t
+        for z in (0, 1):
+            mm(A("M0", 192 * z, 192), A("R32"), A(x, 1664 * z + 192, 192))
+        act(A("SV"), A("M0", 0, 384), "Copy")
+        tr = []
+        for z in (0, 1):
+            tr.append((A(x, 1664 * z + 1280, 192), A(x, 1664 * z, 192)))
+            tr.append((A(x, 1664 * z + 1472, 192), A("SV", 192 * z, 192)))
+        s = add("G", "rem", [], [b for a, b in tr], 1.0, tr=tr, sem="av%d" % t, lat=2.5)
+        add("R", "arr", [A(x, 1280, 384), A(x, 2944, 384)], [], 0.0, sem="av%d" % t, ntr=4, after=s, lat=1.0)
+
+    def names(par):
+        nm = A("NM%d" % par)
+        act(nm, IND(A("TF"), A("HU", 12 * par, 12)), "Copy")
+        cp(A("NU%d" % par), nm)
+        act(A("SG%d" % par), nm, "Sign", 1279.5, -1.0)
+
+    send_sides(0)
+    view_lists(0, 24)
+    views(0, 0, 24, True)
+    send_views(0)
+    mm(A("M0", 0, 384), A("RR", 256, 128, p=(0, 24)), A("XG", 0, 384, p=(0, 24)))
+    for par in (0, 1):
+        tt(A("PR"), A("M0", par, 192, 2), A("DG"), "mul")
+        scan(A("S1"), A("KEEP"), A("PR"), 0.0, "mul", "add")
+        ts(A("HL", 12 * par, 12), A("S1", 15, 12, 16), 192.0, "add")
+        cp(A("HU", 12 * par, 12), A("S1", 15, 12, 16))
+    names(0)
+    view_lists(24, 80)
+    views(0, 24, 80)
+
+    def host_out(par):
+        mm(A("M0", 0, 128, p=(0, 12)), A("HL", 12 * par, 12), A("I32"))
+        act(A("YH", par, 128, 2, p=(0, 12)), A("M0", 0, 128, p=(0, 12)), "Identity", A("TH", 2, 1, p=(0, 12)))
+
+    ms(col("TH", 2), -192.0)
+    ms(col("TH", 3), 2.0 ** -6)
+    turn = [0]
+    for t in range(RO):
+        par, last, mark = t % 2, t == RO - 1, {}
+        x, sd, nm = "X%d" % t, "SD%d" % t, "NM%d" % par
+        if not last:
+            dma("Y", A("SD%d" % (t + 1), 192, 1280), A(sd, 192, 1280), 3.3e5)
+        mm(A("M1", 0, 320), A("I32"), A("TF", t, 320, 4), True, False)
+        mm(A("M1", 0, 320), A("IB"), A(sd, 192 + t, 320, 4), False, True)
+        cp(A("TI"), A("M1", 0, 320))
+        act(A("UC" if t else "UB"), A("UW", 192 + t, 320, 4), "Copy", 0.0, -1.0)
+        for h in range(3):
+            m, el = "M%d" % (h % 2), A("EL", 64 * h, 64)
+            eo, ei = A("EB", 1024 * h, 1024), IND(A(sd, 192, 1664), A("NU%d" % par, 64 * h, 64))
+            if h in cfg["ev"]: cp(eo, ei)
+            else: act(eo, ei, "Copy")
+            for b in range(16):
+                mm(A(m, 0, 64), A("DB", 128 * b, 128), A("EB", 1024 * h + b, 64, 16), b == 0, b == 15)
+            act(el, A(m, 0, 64), "Sign")
+            for hf in (0, 1):
+                o = A(m, 192 + 32 * hf, 32)
+                mm(o, A("I32"), A("KW", 96 * par + 32 * h, 32), True, False)
+                for sg in (0, 1):
+                    mm(o, A("PB", 128 * (2 * hf + sg), 128), A("EL", 64 * h + sg, 32, 2), False, sg == 1)
+            if h in cfg["wf"]: cp(A("IX", 192 * h, 64), A(m, 192, 64))
+            for hf in (0, 1):
+                o = A(m, 256 + 32 * hf, 32)
+                for sg in (0, 1):
+                    mm(o, A("PM", 128 * (2 * hf + sg), 128), A(nm, 64 * h + sg, 32, 2), sg == 0, False)
+                for sg in (0, 1):
+                    mm(o, A("PK", 128 * (2 * hf + sg), 128), A("EL", 64 * h + sg, 32, 2), False, sg == 1)
+            for li in (0, 1):
+                o = A(m, 320 + 32 * li, 32)
+                mm(o, A("I32"), A("KA", 48 * li, 32), True, False)
+                for sg in (0, 1):
+                    mm(o, A("WA", 128 * (2 * li + sg), 128), A("EL", 64 * h + sg, 32, 2), False, sg == 1)
+            o = 64 if h in cfg["wf"] else 0
+            cp(A("IX", 192 * h + o, 192 - o), A(m, 192 + o, 192 - o))
+            mark["w%d" % h] = act(A("WS%d" % h), IND(A("UW", 1472, 768), A("IX", 192 * h, 64)), "Copy")
+            tt(A("D%d" % h), IND(A(x), A("IX", 192 * h + 64, 64)), A("WS%d" % h), "sub")
+        sgn = A("SG%d" % par)
+        mm(A("M0", 0, 192), A("IB"), A("EL"), True, False)
+        mm(A("M0", 0, 192), A("IH"), sgn, False, True)
+        mm(A("M0", 192, 192), A("IN1"), A("EL"), True, False)
+        mm(A("M0", 192, 192), A("IH"), sgn, False, True)
+        act(A("FIT", 0, 192), A("M0", 0, 192), "Relu", -0.5)
+        act(A("FIT", 192, 192), A("M0", 192, 192), "Relu", 0.5)
+        for z in (0, 1):
+            mm(A("M0", 192 * z, 192), A("MT"), A("FIT", 192 * z, 192), True, False)
+            mm(A("M0", 192 * z, 192), A("IK"), A("FIT", 192 * z, 192), False, False)
+            mm(A("M0", 192 * z, 192), A("I32"), A(nm), False, True)
+        act(A("VAL"), A("M0", 0, 384), "Relu", 192.0 - 2048.0)
+        mm(A("M0", 0, 384), A("BO32"), A("VAL"))
+        act(A("CAND"), A("M0", 0, 384), "Copy")
+
+        def scale(r):
+            if cfg["ss"]: act(r, r, "Copy", 0.0, 2.0 ** -6)
+            else: ts(r, r, 2.0 ** -6, "mul")
+
+        def shock(h, p):
+            d, q, bb = "D%d" % h, "QW%d" % h, "WS%d" % h
+            act(A(p), A(d), "Abs")
+            tt(A(q, 512, 1024), A(d), A(p), "mul")
+            lo, hi, o = A(q, 512, 512), A(q, 1024, 512), A(q, 1536, 512)
+            if h in cfg["pes"]:
+                mm(A(p, 0, 512), A("I32"), lo, True, False)
+                mm(A(p, 0, 512), A("I32"), hi, False, True)
+                if cfg["sv"]: cp(o, A(p, 0, 512))
+                else: act(o, A(p, 0, 512), "Copy")
+            else:
+                tt(o, lo, hi, "add")
+            mark["a%d" % h] = act(A(bb, 512, 512), IND(A(q), A("IX", 192 * h + 160, 32)), "Copy")
+            tt(A(bb, 0, 512), IND(A(q), A("IX", 192 * h + 128, 32)), A(bb, 512, 512), "add")
+            r = A(p, 512, 128)
+            if h in cfg["l3"]:
+                mm(r, A("I32"), A(bb, 0, 128, 4), True, False)
+                mm(r, A("I32"), A(bb, 2, 128, 4), False, True)
+            else:
+                tt(r, A(bb, 0, 128, 4), A(bb, 2, 128, 4), "add")
+            tt(A(d, 0, 128), A(bb, 1, 128, 4), A(bb, 3, 128, 4), "add")
+            tt(r, r, A(d, 0, 128), "add")
+            scale(r)
+            for z in (0, 1):
+                w = A("UW", 1472 + 256 * h + 2 * par + z, 64, 4)
+                tt(w, w, A(p, 512 + z, 64, 2), "add")
+
+        def node(ci, p):
+            n, j0 = 64, 64 * ci
+            d, q, xg = "DA%d" % (ci % 2), "QS%d" % (ci % 2), 1024 * (ci % 3)
+            u = A("UC", j0, n)
+            xb = "EB" if t == 0 else "XG"
+            k = act(A(xb, xg, 1024), IND(A(x), A("TI", j0, n)), "Copy")
+            if ci in cfg["xg"] and cfg["xg"][ci] in mark: ops[k]["after"] = mark[cfg["xg"][ci]]
+            if t == 0 or ci in cfg["psub"]:
+                for k in range(16):
+                    mm(A(p, k * n, n), A("I32" if t else "IB"), A(xb, xg + k, n, 16), True, False)
+                    mm(A(p, k * n, n), A("I32" if t else "IB"), u if t else A("UB", j0, n), False, True)
+                act(A(d), A(p), "Abs")
+            else:
+                if cfg["us"]: act(A(p, 0, n), u, "Copy")
+                else: cp(A(p, 0, n), u)
+                for k in range(16):
+                    tt(A(d, k * n, n), A("XG", xg + k, n, 16), A(p, 0, n), "add")
+                act(A(p), A(d), "Abs")
+            tt(A(q, 0, 8 * n), A(d, 0, 8 * n), A(p, 0, 8 * n), "mul")
+            if cfg["pea"]:
+                o = 0
+                tt(A(q, 12 * n, 4 * n), A(d, 12 * n, 4 * n), A(p, 12 * n, 4 * n), "mul")
+                mm(A(p, 0, 4 * n), A("I32"), A(q, 4 * n, 4 * n), True, False)
+                mm(A(p, 0, 4 * n), A("I32"), A(q, 12 * n, 4 * n), False, True)
+                tt(A(p, 8 * n, 4 * n), A(p, 8 * n, 4 * n), A(d, 8 * n, 4 * n), "mul")
+            else:
+                o = 12 * n
+                tt(A(p, 8 * n, 8 * n), A(p, 8 * n, 8 * n), A(d, 8 * n, 8 * n), "mul")
+                tt(A(p, o, 4 * n), A(p, o, 4 * n), A(q, 4 * n, 4 * n), "add")
+            tt(A(q, 0, 4 * n), A(q, 0, 4 * n), A(p, 8 * n, 4 * n), "add")
+            tt(A(q, 0, 2 * n), A(q, 0, 2 * n), A(p, o, 2 * n), "add")
+            tt(A(p, o + 2 * n, 2 * n), A(p, o + 2 * n, 2 * n), A(q, 2 * n, 2 * n), "add")
+            tt(A(q, 0, n), A(q, 0, n), A(p, o + 2 * n, n), "add")
+            r = A(p, o + 3 * n, n)
+            tt(r, r, A(q, n, n), "add")
+            tt(r, r, A(q, 0, n), "add")
+            un = A("UW", 192 + t + 4 * j0, n, 4)
+            if ci < 2 or last: scale(r)
+            else: tt(r, r, A("MK", j0 - 128, n), "mul")
+            tt(un, un, r, "add")
+
+        done = []
+
+        def units(us):
+            for kind, ci in us:
+                (shock if kind == "s" else node)(int(ci), "P%d" % (turn[0] % 3))
+                turn[0] += 1
+                done.append(kind + ci)
+
+        units(cfg["lastA"] if last else cfg["A"])
+        if not last:
+            names(1 - par)
+        else:
+            dma("Y", ("ys", ALL), A("UW", 1472, 768), 4e5)
+        w0, w1 = A("UW", 1472 + 2 * par, 192, 4), A("UW", 1473 + 2 * par, 192, 4)
+        tt(A("DD"), w0, w1, "sub")
+        ts(A("CMP", 0, 192), A("DD"), col("TH", 4), "gt", 0.59375, "sub")
+        ts(A("CMP", 192, 192), A("DD"), col("TH", 1), "lt", 0.59375, "sub")
+        mm(A("M1", 0, 384), A("BOK"), A("CMP"))
+        tt(A("MM"), A("M1", 0, 384), A("CAND"), "min")
+        tt(A("VV"), A("MM", 0, 192), A("MM", 192, 192), "max")
+        tt(A("PR"), A("VV"), A("DG"), "mul")
+        scan(A("S1"), A("KEEP"), A("PR"), 0.0, "mul", "add")
+        o = 0
+        for c in range(12):
+            n = 192 - 16 * c
+            ts(A("EQ", o, n), A("VV", 16 * c, n), col("S1", 16 * c + 15), "eq", col("WT", 16 * c + 15), "mul")
+            mm(A("M0", 16 * c, n), A("BOB"), A("EQ", o, n), c == 0, c == 11)
+            o += n
+        tt(A("MW", 0, 192), A("M1", 0, 192), w0, "min")
+        tt(A("MW", 192, 192), A("M1", 192, 192), w1, "min")
+        ts(A("DN", 0, 192), A("M1", 192, 192), 0.0, "gt", 1664.0, "mul")
+        act(A("DN", 192, 192), A("DN", 0, 192), "Sign")
+        tt(A("M0", 0, 192), A("M0", 0, 192), A("THR"), "lt")
+        tt(A("PR"), A("M0", 0, 192), A("VV"), "mul")
+        scan(A("S2"), A("TD"), A("PR"), 1e6, "min", "max")
+        pos, pu = A("S2", 15, 12, 16), A("PU")
+        cp(pu, pos)
+        if not last:
+            cp(IND(A("SD%d" % (t + 1), 0, 1472), pu), A("DN", 0, 192))
+            send_sides(t + 1)
+        tt(IND(A("C"), pu), A("DN", 192, 192), A("W2S", par, 192, 2), "add")
+        hl, ha = A("HL", 12 * par, 12), A("HA", 0, 12)
+        ts(ha, pos, 192.0, "lt", 4096.0, "mul")
+        tt(ha, ha, hl, "min")
+        tt(hl, ha, pos, "max")
+        if t < 2:
+            ts(A("HU", 12 * par, 12), hl, -192.0, "add")
+        else:
+            host_out(par)
+        if not last:
+            view_lists(0, 80)
+        else:
+            dma("Y", ("yc", ALL), {"b": "C", "lo": 192, "n": 1280, "st": 1, "p": (0, 128, 16)}, 4e4)
+            for gq in range(8):
+                dma("YS"[gq % 2], ("yh", (gq, slice(None))), A("YH", 32 * gq, 32, p=(0, 12)), 2e3)
+        units([k for k in ("n0", "n1") if k not in done])
+        if not last:
+            tt(IND(A("UW", 0, 1472), pu), A("MW", 0, 192), A("MW", 192, 192), "max")
+            views(t + 1, 0, 24, "g" in cfg["vv"])
+            send_views(t + 1)
+            mm(A("M0", 0, 192), A("IB"), A("SD%d" % (t + 1), 192 + t + 512, 192, 4), True, False)
+            mm(A("M0", 0, 192), A("IN1"), A(sd, 192 + t + 512, 192, 4), False, True)
+            act(A("MK"), A("M0", 0, 192), "Abs")
+            act(A("MK"), A("MK"), "Relu", col("TH", 3), -1.0)
+            for k, c0, c1 in (("n2", 24, 48), ("n3", 48, 64), ("n4", 64, 80)):
+                units([k])
+                views(t + 1, c0, c1, k in cfg["vv"])
+        else:
+            units([k for k in ("n2", "n3", "n4") if k not in done])
+            tt(IND(A("UW", 0, 1472), pu), A("MW", 0, 192), A("MW", 192, 192), "max")
+            dma("Y", ("yu", (slice(None), slice(0, 640))), A("UW", 192, 640), 3.3e5)
+            dma("S", ("yu", (slice(None), slice(640, 1280))), A("UW", 832, 640), 3.3e5)
+    return ops
+
+
+ASYNC = ("dma", "rem", "arr")
+HOP = 0.1
+
+
+def plan(cfg):
+    ops = build_ops(cfg)
+    hist = {}
+    for i, o in enumerate(ops):
+        dep = {}
+        for acc, w in ((o["rd"], False), (o["wr"], True)):
+            for s in acc:
+                b, lo, hi = s[:3]
+                for s2, j, w2 in hist.get(b, ()):
+                    if b in PS and ops[j]["e"] != o["e"]:
+                        if lo // 512 <= (s2[2] - 1) // 512 and s2[1] // 512 <= (hi - 1) // 512: dep[j] = True
+                    elif (w or w2) and o["k"] != "arr" and meet(s, s2):
+                        dep[j] = dep.get(j, False) or not (b in PS and o.get("acc"))
+        if o["k"] == "mm":
+            b, lo = o["wr"][0][:2]
+            for s2, j, w2 in hist.get(b, ()):
+                if w2 and ops[j]["k"] == "mm" and s2[1] // 512 == lo // 512 and j not in dep: dep[j] = False
+        if "after" in o: dep.setdefault(o["after"], False)
+        o["dep"] = dep
+        for acc, w in ((o["rd"], False), (o["wr"], True)):
+            for s in acc:
+                h = hist.setdefault(s[0], [])
+                if w and s[3] == 1 and s[4] == (0, 128) and o["k"] != "arr" and not o.get("acc"):
+                    h[:] = [r for r in h if not (s[1] <= r[0][1] and r[0][2] <= s[2] and dep.get(r[1]))]
+                h.append((s, i, w))
+    n = len(ops)
+    pri = [0.0] * n
+    for i in range(n - 1, -1, -1):
+        pri[i] += ops[i]["cost"] + ops[i]["lat"]
+        for j in ops[i]["dep"]:
+            pri[j] = max(pri[j], pri[i] + HOP)
+    r = cfg["seed"]
+    for i in range(n):
+        r = (r * 1103515245 + 12345) % 2147483648
+        pri[i] += cfg["noise"] * r / 2147483648
+    pred, succ = [[] for _ in range(n)], [[] for _ in range(n)]
+    for i, o in enumerate(ops):
+        for j, hard in o["dep"].items():
+            d = ops[j]["lat"] + HOP if (hard or o["k"] == "arr") else 0.0
+            pred[i].append((j, d))
+            succ[j].append((i, d))
+    cost, eng = [o["cost"] + 1e-6 for o in ops], [o["e"] for o in ops]
+
+    def place(seq, before, rel):
+        st = [0.0] * n
+        busy = {e: [] for e in "VSTGYR"}
+        for i in seq:
+            s = rel[i]
+            for j, d in before[i]:
+                x = st[j] + cost[j] + d
+                if x > s: s = x
+            b = busy[eng[i]]
+            lo, hi = 0, len(b)
+            while lo < hi:
+                m = (lo + hi) // 2
+                if b[m][1] <= s: lo = m + 1
+                else: hi = m
+            while lo < len(b) and b[lo][0] < s + cost[i]:
+                s = b[lo][1]
+                lo += 1
+            b.insert(lo, (s, s + cost[i]))
+            st[i] = s
+        return st
+
+    zero, lats = [0.0] * n, [o["lat"] for o in ops]
+    top = [0.0] * n
+    for i in range(n - 1, -1, -1):
+        top[i] = max([pri[i]] + [top[k] + 1e-9 for k, d in succ[i]])
+    seq = sorted(range(n), key=lambda i: -top[i])
+    best = None
+    for it in range(cfg["fb"]):
+        iss = place(seq, pred, zero)
+        end = max(iss[i] + cost[i] + lats[i] for i in range(n))
+        if best is None or end < best[0]: best = (end, iss)
+        back = place(sorted(range(n), key=lambda i: -(iss[i] + cost[i])), succ, lats)
+        seq = sorted(range(n), key=lambda i: -(back[i] + cost[i]))
+    for it in range(cfg["ls"]):
+        key = list(best[1])
+        r = (r * 1103515245 + 12345) % 2147483648
+        t0, amp = best[0] * r / 2147483648, (0.5, 1.5, 3.0)[it % 3]
+        for i in range(n):
+            if t0 - 8 < key[i] < t0 + 8:
+                r = (r * 1103515245 + 12345) % 2147483648
+                key[i] += amp * (r / 2147483648 - 0.5)
+            for j, d in pred[i]:
+                if key[j] >= key[i]: key[i] = key[j] + 1e-7
+        iss = place(sorted(range(n), key=lambda i: key[i]), pred, zero)
+        back = place(sorted(range(n), key=lambda i: -(iss[i] + cost[i])), succ, lats)
+        iss = place(sorted(range(n), key=lambda i: -(back[i] + cost[i])), pred, zero)
+        end = max(iss[i] + cost[i] + lats[i] for i in range(n))
+        if end <= best[0]: best = (end, iss)
+    iss = best[1]
+    fin = [iss[i] + cost[i] + lats[i] for i in range(n)]
+    order = sorted(range(n), key=lambda i: iss[i])
+    ready = "VSTGYR"
+    cnt = {e: 0 for e in ready}
+    know = {e: {} for e in ready}
+    nd = 0
+    for i in order:
+        o = ops[i]
+        kn = know[o["e"]]
+        waits = {}
+        for j, hard in o["dep"].items():
+            if hard and kn.get(ops[j]["id"][0], 0) < ops[j]["id"][1]:
+                s, v = ops[j]["id"]
+                if v > waits.get(s, (0, 0))[0]: waits[s] = (v, j)
+        todo = sorted(waits.items(), key=lambda w: -fin[w[1][1]])
+        o["waits"] = []
+        for s, (v, j) in todo:
+            if kn.get(s, 0) >= v: continue
+            o["waits"].append((s, v))
+            kn[s] = v
+            for s2, v2 in ops[j]["clock"].items():
+                if kn.get(s2, 0) < v2: kn[s2] = v2
+        if o["k"] == "arr":
+            o["id"], o["clock"] = (o["sem"], 1), {}
+        elif o["k"] in ASYNC:
+            o["id"], o["clock"] = ("d%d" % nd, 1), dict(kn)
+            nd += 1
+        else:
+            cnt[o["e"]] += 1
+            o["id"], o["clock"] = ("c" + o["e"], cnt[o["e"]]), dict(kn)
+    return ops, order, cnt, nd, iss, fin
+
+
+OPS, ORDER, CNT, NDMA, ISS, FIN = plan(CFG)
+SEMAPHORES = ["cV", "cS", "cT", "cG"] + ["d%d" % k for k in range(NDMA)] + ["as%d" % t for t in range(RO)] + ["av%d" % t for t in range(RO)]
+ALU = {"add": AluOpType.add, "sub": AluOpType.subtract, "mul": AluOpType.mult, "max": AluOpType.max, "min": AluOpType.min,
+       "ge": AluOpType.is_ge, "gt": AluOpType.is_gt, "lt": AluOpType.is_lt, "eq": AluOpType.is_equal,
+       "and": AluOpType.bitwise_and, "shr": AluOpType.arith_shift_right}
+FUN = {"Copy": ActivationFunctionType.Copy, "Identity": ActivationFunctionType.Identity, "Abs": ActivationFunctionType.Abs,
+       "Sign": ActivationFunctionType.Sign, "Relu": ActivationFunctionType.Relu}
+
+
+def rank_program(g, core, T, topo):
+    rank = T.rank_of(core)
+    if rank is None:
+        return
+    n = len(T.cores)
+    dst, src = T.cores[(rank - 1) % n], T.cores[(rank + 1) % n]
+    rid, pid, _ = topo.addr(dst)
+    eout, ein = topo.engines(core, dst), topo.engines(src, core)
+    Q = {"V": g.vector, "S": g.scalar, "T": g.tensor, "G": g, "Y": g.sync}
+
+    def ap(a):
+        if isinstance(a, tuple): return T[a[0]][a[1]]
+        if not isap(a): return a
+        if "off" in a:
+            return T[a["b"]][:, a["lo"]:a["lo"] + a["wn"]].indirect(ap(a["off"]))
+        cs = slice(a["lo"], a["lo"] + (a["n"] - 1) * a["st"] + 1, a["st"]) if a["st"] > 1 else slice(a["lo"], a["lo"] + a["n"])
+        return T[a["b"]][slice(*a["p"]), cs]
+
+    full = {}
+    for o in OPS:
+        if o["k"] == "arr": full[o["id"][0]] = len(ein) // o["ntr"] * o["ntr"]
+        elif o["k"] == "rem": full[o["id"][0]] = len(eout) // len(o["tr"]) * len(o["tr"])
+        elif o["k"] == "dma": full[o["id"][0]] = 16
+    for i in ORDER:
+        o = OPS[i]
+        k = o["k"]
+        if k == "arr": continue
+        q = Q[o["e"]]
+        for s, v in o["waits"]:
+            q.wait_ge(T.sem[s], v * full.get(s, 1))
+        sem = T.sem[o["id"][0]]
+        if k == "rem":
+            per = len(eout) // len(o["tr"])
+            if len(o["tr"]) == 1:
+                g.remote_dma(ap(o["tr"][0][0]), ap(o["tr"][0][1]), T.sem[o["sem"]], sem, pid, rid, topo.mask(core, dst))
+            else:
+                g.remote_dma_fused([RemoteDMATransfer(dst_ids=[DstId(rid=rid, pnc=pid)], dma_engine_mask=sum(1 << e for e in eout[m * per:(m + 1) * per]),
+                                                      remote_sem=T.sem[o["sem"]], src=ap(b), dst=ap(a)) for m, (a, b) in enumerate(o["tr"])], local_sem=sem)
+            continue
+        a = o["a"]
+        if k == "dma":
+            q.dma_start(ap(a[0]), ap(a[1])).then_inc(sem, 16)
+            continue
+        if k == "tt": r = q.tensor_tensor(ap(a[0]), ap(a[1]), ap(a[2]), ALU[a[3]])
+        elif k == "ts":
+            if a[5] is None: r = q.tensor_scalar(ap(a[0]), ap(a[1]), ap(a[2]), None, ALU[a[4]])
+            else: r = q.tensor_scalar(ap(a[0]), ap(a[1]), ap(a[2]), ap(a[3]), ALU[a[4]], ALU[a[5]])
+        elif k == "cp": r = q.tensor_copy(ap(a[0]), ap(a[1]))
+        elif k == "ms": r = q.memset(ap(a[0]), a[1])
+        elif k == "scan": r = q.tensor_tensor_scan(ap(a[0]), ap(a[1]), ap(a[2]), a[3], ALU[a[4]], ALU[a[5]])
+        elif k == "act": r = q.activation(ap(a[0]), ap(a[1]), FUN[a[2]], bias=ap(a[3]), scale=ap(a[4]))
+        elif k == "mm": r = q.matmul(ap(a[0]), ap(a[1]), ap(a[2]), a[3], a[4])
+        elif BUF[a[0]["b"]][1] == I: r = q.iota(ap(a[0]), a[1], a[2], a[3])
+        else: r = q.iota(ap(a[0]), a[1], a[2], a[3], allow_small_or_imprecise_dtypes=True)
+        r.then_inc(sem, 1)
+    for e in "VSTG":
+        g.wait_ge(T.sem["c" + e], CNT[e])
+    for s, v in full.items():
+        g.wait_ge(T.sem[s], v)

@@ -2,33 +2,38 @@ import math
 from concourse.bass import DstId, RemoteDMATransfer
 from concourse.mybir import AluOpType, ActivationFunctionType
 
-CFG = {"A": ["s0", "s1", "s2"], "lastA": ["s0", "s1", "s2"],
-       "pes": (0,), "pea": False, "l3": (), "wf": (0,), "ss": True, "us": True, "sv": False, "ev": (1,),
-       "psub": (0, 2, 4), "xg": {}, "vv": ("g", "n4"), "fb": 3, "ls": 1200, "seed": 0, "noise": 0.0}
+CFG = {"vg": "early", "vra": None, "cl": 3, "pair": "svs", "c1": (), "one": True, "cb": "SL", "vr": ((24, 52), (52, 80)),
+       "half": (0, 1, 2), "ev": ((1,), (1,), (1,), (1,)), "dd": "T", "vv": ("r", "", "", ""),
+       "pe": ("a0", "a1 a3 b0 b2", "a1 a3 b0 b2", "a1 a3 b0 b2 b1"), "tree": ("abc", "abc", "abc", "abc"), "rot": "Y",
+       "run": 0.9, "fbe": 5, "heat": 0.15, "all": 100, "ls": 170, "wide": 16, "steps": 300, "slack": 0.0, "seed": 0}
 RO = 4
-F, B, I, U = "float32", "bfloat16", "int32", "uint16"
+F, B, H, I, U = "float32", "bfloat16", "float16", "int32", "uint16"
 BUF = {
-    "UW": (2240, F), "C": (1472, F), "TL": (1280, I), "IN": (1280, I), "XG": (3072, F), "TH": (8, F),
+    "UW": (3392, F), "C": (1472, F), "TL": (1280, I), "IN": (1280, I), "U0B": (2432, B), "XC": (1280, H), "TH": (8, F),
+    "WN": (384, F), "XL0": (384, U), "XL1": (384, U), "SO": (384, F), "SOB": (384, B),
     "D0": (1024, F), "D1": (1024, F), "D2": (1024, F), "WS0": (1024, F), "WS1": (1024, F), "WS2": (1024, F),
-    "DA0": (1024, F), "DA1": (1024, F), "QS0": (1024, F), "QS1": (1024, F), "QW0": (2048, F), "QW1": (2048, F), "QW2": (2048, F), "R32": (128, F),
-    "PM": (512, F), "PB": (512, B), "PK": (512, B), "KW": (192, F),
-    "EB": (3072, B), "EL": (192, B), "IX": (576, U), "NM0": (192, F), "NM1": (192, F), "NU0": (192, U), "NU1": (192, U),
-    "SG0": (192, B), "SG1": (192, B), "FIT": (384, B), "VAL": (384, F), "CAND": (384, F),
-    "TI": (320, U), "TF": (1280, F), "UC": (320, F), "UB": (320, B), "MK": (192, F), "HL": (24, F), "HU": (24, U), "HA": (24, F), "YH": (256, F),
-    "DD": (192, F), "CMP": (384, B), "MM": (384, F), "VV": (192, F), "PR": (192, F), "S1": (192, F), "S2": (192, F),
-    "EQ": (1248, B), "PU": (12, U), "MW": (384, F), "DN": (384, F),
-    "CI": (160, I), "VA": (160, F), "VL": (160, U), "ST": (384, B), "SV": (384, F),
-    "IK": (128, B), "JF": (192, F), "JG": (128, F), "PI": (8, I), "PF": (16, F), "OH": (16, F), "T1": (192, F), "T2": (192, F), "TJ": (192, F),
-    "I32": (128, F), "IB": (128, B), "IH": (128, B), "IN1": (128, B), "ROT": (128, B),
-    "BO32": (128, F), "BOB": (128, B), "BOK": (128, B), "MT": (128, B), "WA": (512, B), "RR": (384, F),
-    "D32": (2048, F), "DB": (2048, B), "DG": (192, F), "KEEP": (192, F), "TD": (192, F), "THR": (192, F), "WT": (192, F),
-    "W2S": (384, F), "KA": (96, F), "ML": (160, F),
+    "QW0": (2048, F), "QW1": (2048, F), "R32": (128, F),
+    "ND0": (512, F), "ND1": (512, F), "ND2": (512, F), "QN0": (1536, F), "QN1": (1536, F), "XG0": (512, F), "XG1": (512, F),
+    "XB": (2048, B), "UR": (1280, F), "IQ": (128, B), "TS": (1536, H), "REP": (320, B), "SLT": (128, B), "T3": (320, F),
+    "PM": (512, H), "PB": (512, B), "PK": (512, B), "KW": (128, B), "KA": (128, B),
+    "EB": (3072, B), "EL": (192, B), "IX": (384, U), "NM0": (192, H), "NM1": (192, H),
+    "GH0": (192, B), "GH1": (192, B), "FIT": (384, B), "VAL": (384, F), "CAND": (384, F),
+    "TI0": (320, U), "TI1": (320, U), "TF": (1280, H), "MK": (192, F), "SN": (192, B), "HL": (24, F), "HU": (24, U), "HA": (24, F), "YH": (256, F),
+    "DD": (192, F), "CMP": (384, B), "MM": (384, F), "VV": (192, H), "PR": (192, F), "S1": (192, F), "S2": (192, F),
+    "EQ": (1248, B), "PU": (12, U), "MW": (384, F), "DN": (192, F),
+    "VA": (160, F), "VL": (160, U), "ST": (384, B), "SV": (384, F), "SVB": (384, B),
+    "IK": (128, B), "JF": (192, F), "JG": (128, F), "PI": (8, I), "PF": (20, F), "OH": (16, F), "T1": (192, F), "T2": (192, F), "TJ": (192, F),
+    "I32": (128, F), "N32": (128, F), "IB": (128, B), "I16": (128, H), "IN1": (128, B), "ROT": (128, B),
+    "BO32": (128, F), "BOB": (128, B), "BOK": (128, B), "MT": (128, B), "WA": (512, B), "RR": (384, H),
+    "D32": (2048, F), "DB": (2048, B), "DG": (192, F), "KEEP": (192, F), "TD": (192, F), "THR": (192, B), "BOI": (128, B),
+    "W2S": (384, F), "ML": (160, F),
 }
 for _t in range(RO):
-    BUF["X%d" % _t] = (3328, F)
+    BUF["X%d" % _t] = (3328, F if _t else B)
     BUF["SD%d" % _t] = (1856, B)
-PS = {"P0": 1024, "P1": 1024, "P2": 1024, "M0": 512, "M1": 512}
-ALIAS = {"RR": "MW", "VAL": "MM", "JG": "VV", "TJ": "DN", "T1": "MK", "T2": "UC"}
+PS = {"SA": 512, "SB": 512, "SL": 512, "NA": 512, "NB": 512, "NC": 512, "M0": 512, "M1": 512}
+ALIAS = {"VAL": "MM", "JG": "WN", "TJ": "DN", "T1": "MK", "T2": "CAND", "JF": "SO", "YH": "X1", "VV": "RR", "SN": "ST", "T3": "ND0", "SVB": "FIT", "SOB": "CMP", "DD": "S2"}
+CHUNK = {"a": (0, 128), "b": (128, 128), "c": (256, 64)}
 SCRATCH = {k: ("sbuf", [128, v[0]], v[1]) for k, v in BUF.items() if k not in ALIAS}
 for _k, _v in PS.items():
     SCRATCH[_k] = ("psum", [128, _v], F)
@@ -81,7 +86,7 @@ def build_ops(cfg):
         return 0.02 + max(64, n * c) * 0.00083
 
     def two(*a):
-        return all(x["b"] in BUF and BUF[x["b"]][1] in (B, U) for x in a)
+        return all(x["b"] in BUF and BUF[x["b"]][1] in (B, H, U) for x in a)
 
     def tt(o, a, b, op):
         c = 1 if (a["b"] in PS or b["b"] in PS) else 2
@@ -104,38 +109,57 @@ def build_ops(cfg):
 
     def mm(o, l, r, start=True, stop=True):
         w = 4 if BUF[r["b"]][1] == F else 1
-        return add("T", "mm", [o], [l, r] + ([] if start else [o]), 0.01 + max(64, r["n"]) * w * 0.00042, a=(o, l, r, start, stop), acc=not start)
+        k = add("T", "mm", [o], [l, r] + ([] if start else [o]), 0.01 + max(64, r["n"]) * w * 0.00042, a=[(o, l, r, start, stop)], acc=not start)
+        a, b = ops[k - 1], ops[k]
+        if not start and a["k"] == "mm" and a["cost"] + b["cost"] < cfg["run"]:
+            for f in ("rd", "wr", "a", "cost"): a[f] += b[f]
+            a["rd"] = [s for s in a["rd"] if a["acc"] or s[0] != o["b"]]
+            ops.pop()
 
     def iota(o, pat, base, cm):
         return add("G", "iota", [o], [], 0.13 + o["n"] * 2 * 0.00083, a=(o, pat, base, cm))
 
-    def dma(q, o, a, nbytes):
-        return add(q, "dma", [o] if isap(o) else [], [a], 1.0 if q == "G" else 0.1, a=(o, a), lat=1.9 + nbytes / 2e5)
+    def gcp(o, a):
+        return add("G", "gcp", [o], [a], 0.17 + o["n"] * 2 * 0.00083, a=(o, a))
+
+    def dma(q, o, a, rows, nbytes):
+        move = max(1, rows / 16) * (ROW + nbytes / RATE)
+        if q == "Y": return add(q, "dma", [o] if isap(o) else [], [a], max(0.1, move), a=(o, a), lat=1.8)
+        return add(q, "dma", [o] if isap(o) else [], [a], 1.0 if q == "G" else 0.1, a=(o, a), lat=1.8 + move)
+
+    def send(sem, tr):
+        size = 4 if BUF[tr[0][0]["b"]][1] == F else 2
+        s = add("G", "rem", [], [b for a, b in tr], 1.0, tr=tr, sem=sem, lat=0.8 + 16 * len(tr) * (ROW + tr[0][0]["n"] * size / RATE))
+        add("R", "arr", [a for a, b in tr], [], 0.0, sem=sem, ntr=len(tr), after=s, lat=0.8)
+        return s
 
     def col(name, c):
         return A(name, c, 1)
 
     ALL = (slice(None), slice(None))
-    dma("Y", A("IN", 0, 1280, p=(0, 8)), ("sd", ALL), 4e4)
-    dma("Y", A("IN", 0, 1280, p=(8, 16)), ("nr", ALL), 4e4)
-    dma("Y", A("IN", 0, 384, p=(16, 24)), ("hs", ALL), 1e4)
-    dma("S", A("EB", 1280, 768), ("w0", ALL), 2e5)
-    dma("S", A("EB", 0, 1280), ("u0", ALL), 3.3e5)
-    dma("Y", A("TL"), ("tl", ALL), 6.6e5)
-    dma("Y", col("TH", 4), ("th", ALL), 1e3)
+    dma("Y", A("IN", 0, 1280, p=(0, 8)), ("sd", ALL), 16, 2560)
+    dma("Y", A("IN", 0, 1280, p=(8, 16)), ("nr", ALL), 16, 2560)
+    dma("Y", A("IN", 0, 384, p=(16, 24)), ("hs", ALL), 16, 768)
+    dma("S", A("U0B", 0, 1280), ("u0", ALL), 128, 2560)
+    dma("S", A("U0B", 1280, 768), ("w0", ALL), 256, 1536)
+    dma("Y", A("TL"), ("tl", ALL), 128, 5120)
+    dma("Y", col("TH", 4), ("th", ALL), 128, 4)
     iota(col("PI", 0), [[0, 1]], 0, 1)
     iota(A("JF"), [[1, 192]], 0, 0)
     iota(A("JG"), [[1, 8], [0, 16]], 0, 0)
     iota(A("TJ"), [[0, 12], [1, 16]], 0, 0)
-    iota(A("W2S"), [[2, 384]], 0, 0)
+    iota(A("W2S"), [[2, 384]], 1281, 0)
     cp(col("PF", 0), col("PI", 0))
     for c, (s, op) in enumerate(((15, "and"), (4, "shr"), (7, "and"), (3, "shr"))):
         ts(col("PI", 1 + c), col("PI", 0), s, op)
     cp(A("PF", 1, 4), A("PI", 1, 4))
     ts(col("PF", 4), col("PF", 4), 1.0, "add")
     ts(col("PF", 5), col("PF", 0), 16.0, "ge")
-    ts(A("RR", 0, 128), A("JG"), col("PF", 3), "eq", col("PF", 4), "mul")
-    ts(A("RR", 128, 128), A("JG"), col("PF", 3), "eq", 1664.0, "mul")
+    ts(col("PF", 16), col("PF", 4), 2.0, "eq", 2.0, "mul")
+    ts(col("PF", 18), col("PF", 4), 1.0, "eq", -0.5, "mul")
+    ts(col("PF", 17), col("PF", 16), 640.5 / 2, "mul", col("PF", 18), "add")
+    ts(A("RR", 0, 128), A("JG"), col("PF", 3), "eq", col("PF", 16), "mul")
+    ts(A("RR", 128, 128), A("JG"), col("PF", 3), "eq", 2.0, "mul")
     ts(A("RR", 256, 128), A("JG"), col("PF", 3), "eq", col("PF", 5), "mul")
     ts(A("I32"), A("JF", 0, 128), col("PF", 0), "eq")
     ts(A("OH"), A("JF", 0, 16), col("PF", 1), "eq")
@@ -145,19 +169,27 @@ def build_ops(cfg):
     act(A("R32", 0, 112), A("I32", 16, 112), "Copy")
     act(A("R32", 112, 16), A("I32", 0, 16), "Copy")
     act(A("ROT"), A("R32"), "Copy")
-    for z in (0, 1):
-        ts(A("ML", 80 * z, 80), A("JF", 0, 80), 16.0, "mul", col("PF", 1), "add")
+    ts(A("ML", 80, 80), A("JF", 0, 80), 16.0, "mul", col("PF", 1), "add")
+    ts(A("ML", 0, 80), A("ML", 80, 80), 1.0, "add")
+    ts(A("ML", 80, 80), A("ML", 80, 80), -1.0, "mul")
     ts(A("DG"), A("TJ"), col("PF", 1), "eq")
     act(A("KEEP"), A("TJ"), "Sign")
-    dma("G", A("DB"), A("D32"), 5e5)
-    act(A("IH"), A("I32"), "Copy", 0.0, 0.5)
+    for b in range(16):
+        ts(A("DB", 128 * b, 128), A("IB"), col("OH", b), "mul")
+    cp(A("I16"), A("IB"))
     act(A("IN1"), A("I32"), "Copy", 0.0, -1.0)
+    act(A("N32"), A("I32"), "Copy", 0.0, -1.0)
+    act(A("IQ"), A("I32"), "Copy", 0.0, 0.25)
+    for c0, w in ((0, 8), (8, 8), (16, 4)):
+        iota(A("T3", 16 * c0, 16 * w), [[0, 16], [1, w]], c0, 0)
+    ts(A("REP"), A("T3"), col("PF", 0), "eq", 0.25, "mul")
     act(A("IK"), A("I32"), "Copy", 0.0, 2048.0)
     ts(A("BO32"), A("JG"), col("PF", 2), "eq")
-    act(A("BOB"), A("BO32"), "Copy")
-    act(A("BOK"), A("BO32"), "Copy", 0.0, 8192.0)
+    act(A("BOB"), A("BO32"), "Copy", 0.0, -2.0 ** 46)
+    act(A("BOK"), A("BO32"), "Copy", 0.0, 4096.0)
     ts(A("T1", 0, 128), A("JF", 0, 128), col("PF", 0), "gt", -2048.0, "mul")
-    tt(A("MT"), A("T1", 0, 128), A("BO32"), "mul")
+    tt(A("T1", 0, 128), A("T1", 0, 128), A("BO32"), "mul")
+    tt(A("MT"), A("T1", 0, 128), A("IK"), "add")
     ts(col("TH", 1), col("TH", 4), -1.0, "mul")
     ts(col("PF", 7), col("PF", 1), 8.0, "ge", 512.0, "mul")
     ts(col("PF", 7), col("PF", 7), 512.0, "add")
@@ -176,95 +208,115 @@ def build_ops(cfg):
     tt(col("PF", 7), col("PF", 7), col("PF", 6), "sub")
     for hf in (0, 1):
         for sg in (0, 1):
-            act(A("PM", 128 * (2 * hf + sg), 128), A("S1", 16 - 8 * sg, 128), "Copy", 0.0, col("PF", 11 - hf))
+            act(A("PB", 128 * (2 * hf + sg), 128), A("S1", 16 - 8 * sg, 128), "Copy", 0.0, col("PF", 11 - hf))
             act(A("WA", 128 * (2 * hf + sg), 128), A("PR", 16 - 8 * sg, 128), "Copy", 0.0, col("PF", 7 - hf))
-    act(A("PB"), A("PM"), "Copy")
-    act(A("PK"), A("PM"), "Copy", 0.0, 1664.0)
-    ts(A("KW", 0, 96), A("JF", 0, 96), 8.0, "mul", col("PF", 13), "add")
-    ts(A("KW", 96, 96), A("KW", 0, 96), 2.0, "add")
+    cp(A("PM"), A("PB"))
+    act(A("PK"), A("PB"), "Copy", 0.0, 384.0)
+    iota(A("SV", 0, 128), [[2, 2], [0, 2], [8, 32]], 0, 0)
+    iota(A("SV", 128, 64), [[0, 2], [16, 32]], 0, 0)
+    iota(A("SV", 192, 64), [[4, 2], [0, 32]], 0, 0)
+    ts(A("KW"), A("SV", 0, 128), col("PF", 13), "add")
     ts(col("PF", 9), col("PF", 9), -1536.0, "mul", 1536.0, "add")
     ts(col("PF", 14), col("PF", 10), 8.0, "mul", col("PF", 8), "add")
-    tt(col("PF", 14), col("PF", 14), col("PF", 9), "add")
-    ts(A("KA", 0, 48), A("JF", 0, 48), 16.0, "mul", col("PF", 14), "add")
-    ts(A("KA", 48, 48), A("KA", 0, 48), 4.0, "add")
-    ms(A("T1"), 0.5)
-    iota(A("T2"), [[0, 192]], 0, 0)
-    scan(A("PR"), A("T1"), A("T2"), 2.0 ** 97, "mul", "add")
-    tt(A("THR"), A("PR"), A("DG"), "mul")
-    scan(A("PR"), A("KEEP"), A("THR"), 0.0, "mul", "add")
-    act(A("WT"), A("PR"), "Copy", 0.0, 0.5)
-    iota(A("DD"), [[-1, 192]], 191, 0)
-    ts(A("T2"), A("KEEP"), 1e6, "mul", col("PF", 1), "sub")
-    tt(A("TD"), A("DD"), A("T2"), "add")
-    for b in range(3):
+    ts(A("KA", 0, 64), A("SV", 128, 64), col("PF", 9), "add")
+    ts(A("KA", 64, 64), A("SV", 192, 64), col("PF", 14), "add")
+    ms(A("HA", 0, 16), 0.5)
+    scan(A("VA", 0, 16), A("HA", 0, 16), A("OH"), 2.0 ** 47, "mul", "max")
+    tt(A("VA", 16, 16), A("VA", 0, 16), A("OH"), "mul")
+    scan(A("VA", 32, 16), A("VA", 16, 16), A("OH"), 0.0, "max", "max")
+    ts(A("THR"), A("DG"), col("VA", 47), "mul")
+    ts(A("BOI"), A("BO32"), col("VA", 47), "mul", -0.5, "mul")
+    ts(col("PF", 19), col("PF", 2), 16.0, "mul")
+    iota(A("T2"), [[-16, 12], [4096, 16]], 191, -1)
+    ts(A("TD"), A("T2"), col("PF", 19), "add")
+    for b in range(2):
         iota(A("QW%d" % b, 0, 512), [[0, 512]], 0, 0)
     for b in ("UW", "C", "SD1", "SD2", "SD3"):
         iota(A(b, 0, 192), [[0, 192]], 0, 0)
-    cp(A("XG", 0, 384, p=(0, 24)), A("IN", 0, 384, p=(0, 24)))
-    cp(A("XG", 384, 896, p=(0, 16)), A("IN", 384, 896, p=(0, 16)))
-    cp(A("TF", 0, 640), A("TL", 0, 640))
-    cp(A("TF", 640, 640), A("TL", 640, 640))
-    act(A("UW", 1472, 768), A("EB", 1280, 768), "Copy")
-    act(A("UW", 192, 384), A("EB", 0, 384), "Copy")
-    act(A("UW", 576, 896), A("EB", 384, 896), "Copy")
+    ts(A("XC", 0, 384, p=(0, 24)), A("IN", 0, 384, p=(0, 24)), A("PF", 17, 1, p=(0, 24)), "add")
+    ts(A("XC", 384, 896, p=(0, 16)), A("IN", 384, 896, p=(0, 16)), A("PF", 17, 1, p=(0, 16)), "add")
+    for lo, n in ((0, 512), (512, 512), (1024, 256)):
+        ts(A("TF", lo, n), A("TL", lo, n), 0.0, "add")
     for k, (lo, n) in enumerate(((0, 384), (384, 512), (896, 384))):
-        mm(A("P%d" % k, 0, n), A("RR", 0, 128, p=(0, 16)), A("XG", lo, n, p=(0, 16)))
-        cp(A("C", 192 + lo, n), A("P%d" % k, 0, n))
-        mm(A("P%d" % k, 512, n), A("RR", 128, 128, p=(0, 8)), A("XG", lo, n, p=(0, 8)))
-        act(A("SD0", 192 + lo, n), A("P%d" % k, 512, n), "Copy")
+        pa, pb = (("SA", "SB"), ("NA", "NB"), ("SA", "NC"))[k]
+        mm(A(pa, 0, n), A("RR", 128, 128, p=(0, 8)), A("XC", lo, n, p=(0, 8)))
+        act(A("SD0", 192 + lo, n), A(pa, 0, n), "Copy")
+        mm(A(pb, 0, n), A("RR", 0, 128, p=(0, 16)), A("XC", lo, n, p=(0, 16)))
+        tt(A("C", 192 + lo, n), A(pb, 0, n), A("SD0", 192 + lo, n), "mul")
 
     def send_sides(t):
         sd = "SD%d" % t
         mm(A("M0", 0, 192), A("IB"), A(sd, 192, 192))
         mm(A("M0", 192, 192), A("ROT"), A(sd, 384, 192))
         act(A("ST"), A("M0", 0, 384), "Copy")
-        s = add("G", "rem", [], [A("ST")], 1.0, tr=[(A(sd, 1472, 384), A("ST"))], sem="as%d" % t, lat=1.5)
-        add("R", "arr", [A(sd, 1472, 384)], [], 0.0, sem="as%d" % t, ntr=1, after=s, lat=1.0)
+        return send("as%d" % t, [(A(sd, 1472, 384), A("ST"))])
+
+    def send_values(t):
+        b, lo, so, land = ("UW", 192, "SO", 2240 + 384 * (t - 1)) if t else ("U0B", 0, "SOB", 2048)
+        if cfg["one"]:
+            mm(A("SL", 0, 192), A("I32" if t else "IB"), A(b, lo, 192))
+            mm(A("SL", 192, 192), A("R32" if t else "ROT"), A(b, lo + 192, 192))
+            act(A(so), A("SL", 0, 384), "Copy")
+            send("ao%d" % t, [(A(b, land, 384), A(so))])
+        else:
+            mm(A("SL", 0, 192), A("R32" if t else "ROT"), A(b, lo + 192, 192))
+            act(A(so, 0, 192), A("SL", 0, 192), "Copy")
+            send("ao%d" % t, [(A(b, land, 192), A(b, lo, 192)), (A(b, land + 192, 192), A(so, 0, 192))])
 
     def view_lists(c0, c1):
         n = c1 - c0
         for b in range(16):
             mm(A("M1", 384 + c0, n), A("D32", 128 * b, 128), A("C", 192 + 16 * c0 + b, n, 16), b == 0, b == 15)
         cl = A("M1", 384 + c0, n)
-        cp(A("CI", c0, n), cl)
-        ts(A("CI", 80 + c0, n), A("CI", c0, n), 1, "and")
         for z in (0, 1):
             v = A("VA", 80 * z + c0, n)
-            ts(v, A("CI", 80 + c0, n), (4096.0, -4096.0)[z], "mul", (1279.0 - 4096.0, 1281.0)[z], "add")
-            tt(v, v, cl, "add")
-        for lo, m in (((0, 160),) if n == 80 else ((c0, n), (80 + c0, n))):
-            tt(A("VA", lo, m), A("VA", lo, m), A("ML", lo, m), "max")
-            cp(A("VL", lo, m), A("VA", lo, m))
+            tt(v, cl, A("ML", 80 * z + c0, n), ("max", "min")[z])
+            ts(A("VL", 80 * z + c0, n), v, -1.0, ("add", "mul")[z])
 
-    def views(t, c0, c1, split=False):
+    def views(t, c0, c1, split=False, after=None):
         for z in (0, 1):
-            o, a = A("X%d" % t, 1664 * z + 16 * c0, 16 * (c1 - c0)), IND(A("UW", 192, 2048), A("VL", 80 * z + c0, c1 - c0))
-            if split and z: cp(o, a)
-            else: act(o, a, "Copy")
+            o, a = A("X%d" % t, 32 * c0 + z, 16 * (c1 - c0), 2), IND(A("UW", 192, 2048) if t else A("U0B", 0, 2048), A("VL", 80 * z + c0, c1 - c0))
+            k = cp(o, a) if split and z else act(o, a, "Copy")
+            if after is not None and ops[k]["e"] == ops[after]["e"]: ops[k]["after"] = after
 
     def send_views(t):
-        x = "X%d" % t
-        for z in (0, 1):
-            mm(A("M0", 192 * z, 192), A("R32"), A(x, 1664 * z + 192, 192))
-        act(A("SV"), A("M0", 0, 384), "Copy")
-        tr = []
-        for z in (0, 1):
-            tr.append((A(x, 1664 * z + 1280, 192), A(x, 1664 * z, 192)))
-            tr.append((A(x, 1664 * z + 1472, 192), A("SV", 192 * z, 192)))
-        s = add("G", "rem", [], [b for a, b in tr], 1.0, tr=tr, sem="av%d" % t, lat=2.5)
-        add("R", "arr", [A(x, 1280, 384), A(x, 2944, 384)], [], 0.0, sem="av%d" % t, ntr=4, after=s, lat=1.0)
+        x, sv = "X%d" % t, "SV" if t else "SVB"
+        if t and cfg["rot"] == "Y":
+            dma("Y", A(sv, p=(0, 112)), A(x, 384, 384, p=(16, 128)), 112, 1536)
+            dma("Y", A(sv, p=(112, 128)), A(x, 384, 384, p=(0, 16)), 16, 1536)
+        else:
+            mm(A("SL", 0, 384), A("R32" if t else "ROT"), A(x, 384, 384))
+            act(A(sv), A("SL", 0, 384), "Copy")
+        return send("av%d" % t, [(A(x, 2560, 384), A(x, 0, 384)), (A(x, 2944, 384), A(sv))])
 
-    def names(par):
-        nm = A("NM%d" % par)
-        act(nm, IND(A("TF"), A("HU", 12 * par, 12)), "Copy")
-        cp(A("NU%d" % par), nm)
-        act(A("SG%d" % par), nm, "Sign", 1279.5, -1.0)
+    def names(t):
+        par, m = t % 2, max(2, t + 1)
+        nm, sg = "NM%d" % par, "GH%d" % par
+        ts(A(nm), IND(A("TL"), A("HU", 12 * par, 12)), 0.0, "add")
+        ts(A(sg), A(nm), 1279.5, "gt")
+        for hf in (0, 1):
+            o = A("M1", 96 * hf, 96)
+            for k in (0, 1):
+                mm(o, A("PM", 128 * (2 * hf + k), 128), A(nm, k, 96, 2), k == 0, False)
+            for k in range(2 * m):
+                mm(o, A("PK", 128 * (2 * hf + k % 2), 128), A(sg, k % 2, 96, 2), False, k == 2 * m - 1)
+        mm(A("M1", 192, 192), A("I16"), A(nm))
+        cp(A("XL%d" % par), A("M1", 0, 384))
 
+    send_values(0)
     send_sides(0)
     view_lists(0, 24)
     views(0, 0, 24, True)
-    send_views(0)
-    mm(A("M0", 0, 384), A("RR", 256, 128, p=(0, 24)), A("XG", 0, 384, p=(0, 24)))
+    sent = send_views(0)
+    ops[dma("G", A("UW", 1472, 768), ("w0", ALL), 128, 3072)]["behind"] = sent
+    ops[dma("G", A("UW", 192, 1280), ("u0", ALL), 128, 5120)]["behind"] = sent
+    def turn_names(blk, behind):
+        w = (8, 8, 4)[blk]
+        for gq in range(8):
+            k = dma("Y", A("TS", 512 * blk + 64 * gq, 64, p=(0, 16 * w)), A("TF", 512 * blk, 64 * w, p=(16 * gq, 16 * gq + 16)), 16 * w, 128)
+            ops[k]["behind"] = behind
+
+    mm(A("M0", 0, 384), A("RR", 256, 128, p=(0, 24)), A("XC", 0, 384, p=(0, 24)))
     for par in (0, 1):
         tt(A("PR"), A("M0", par, 192, 2), A("DG"), "mul")
         scan(A("S1"), A("KEEP"), A("PR"), 0.0, "mul", "add")
@@ -272,181 +324,215 @@ def build_ops(cfg):
         cp(A("HU", 12 * par, 12), A("S1", 15, 12, 16))
     names(0)
     view_lists(24, 80)
-    views(0, 24, 80)
+
+    def ghost_views(t, after=None):
+        view_lists(0, 80)
+        views(t, 0, 24, "g" in cfg["vv"][t], after)
+        send_views(t)
 
     def host_out(par):
-        mm(A("M0", 0, 128, p=(0, 12)), A("HL", 12 * par, 12), A("I32"))
-        act(A("YH", par, 128, 2, p=(0, 12)), A("M0", 0, 128, p=(0, 12)), "Identity", A("TH", 2, 1, p=(0, 12)))
+        mm(A("SL", 0, 128, p=(0, 12)), A("HL", 12 * par, 12), A("I32"))
+        act(A("YH", par, 128, 2, p=(0, 12)), A("SL", 0, 128, p=(0, 12)), "Identity", A("TH", 2, 1, p=(0, 12)))
 
     ms(col("TH", 2), -192.0)
-    ms(col("TH", 3), 2.0 ** -6)
-    turn = [0]
+    turn = {"bank": 0, "nd": 0, "xg": 0, "qn": 0}
+
+    def take(kind, names):
+        turn[kind] += 1
+        return names[turn[kind] % len(names)]
+
     for t in range(RO):
         par, last, mark = t % 2, t == RO - 1, {}
-        x, sd, nm = "X%d" % t, "SD%d" % t, "NM%d" % par
+        x, sd, nm, ti = "X%d" % t, "SD%d" % t, "NM%d" % par, "TI%d" % par
         if not last:
-            dma("Y", A("SD%d" % (t + 1), 192, 1280), A(sd, 192, 1280), 3.3e5)
-        mm(A("M1", 0, 320), A("I32"), A("TF", t, 320, 4), True, False)
-        mm(A("M1", 0, 320), A("IB"), A(sd, 192 + t, 320, 4), False, True)
-        cp(A("TI"), A("M1", 0, 320))
-        act(A("UC" if t else "UB"), A("UW", 192 + t, 320, 4), "Copy", 0.0, -1.0)
-        for h in range(3):
+            dma("Y", A("SD%d" % (t + 1), 192, 1280), A(sd, 192, 1280), 128, 2560)
+        if t:
+            for j0, n in CHUNK.values():
+                gcp(A("UR", 4 * j0, n), A("UW", 192 + t + 4 * j0, n, 4))
+                gcp(A("UR", 4 * j0 + n, n), A("UR", 4 * j0, n))
+                gcp(A("UR", 4 * j0 + 2 * n, 2 * n), A("UR", 4 * j0, 2 * n))
+            for b in range(16):
+                mm(A("NC", 320, 128, p=(0, 20)), A(sd, 192 + t + 4 * b, 20, 64), A("DB", 128 * b, 128), b == 0, b == 15)
+            act(A("SLT", p=(0, 20)), A("NC", 320, 128, p=(0, 20)), "Copy")
+            mm(A("NC", 0, 320), A("SLT", p=(0, 20)), A("REP", p=(0, 20)), True, False)
+            for j0, k in CHUNK.values():
+                mm(A("NC", j0, k), A("TS", 4 * j0 + t, 128, 4, p=(0, k)), A("I16", 0, k, p=(0, k)), False, k == 64)
+            ts(A(ti), A("NC", 0, 320), 2.0, "mul", 0.5, "add")
+        else:
+            mm(A("NC", 0, 320), A("I16"), A("TF", 0, 320, 4), True, False)
+            mm(A("NC", 0, 320), A("IQ"), A(sd, 192, 320, 4), False, True)
+            ts(A(ti), A("NC", 0, 320), 2.0, "mul", 0.5, "add")
+        for h in (2, 1, 0):
             m, el = "M%d" % (h % 2), A("EL", 64 * h, 64)
-            eo, ei = A("EB", 1024 * h, 1024), IND(A(sd, 192, 1664), A("NU%d" % par, 64 * h, 64))
-            if h in cfg["ev"]: cp(eo, ei)
+            eo, ei = A("EB", 1024 * h, 1024), IND(A(sd, 192, 1664), A("XL%d" % par, 192 + 64 * h, 64))
+            if 2 - h in cfg["ev"][t]: cp(eo, ei)
             else: act(eo, ei, "Copy")
             for b in range(16):
                 mm(A(m, 0, 64), A("DB", 128 * b, 128), A("EB", 1024 * h + b, 64, 16), b == 0, b == 15)
-            act(el, A(m, 0, 64), "Sign")
+            act(el, A(m, 0, 64), "Relu")
+            mm(A(m, 192, 64), A("IB"), A("KW", 64 * par, 64), True, False)
             for hf in (0, 1):
-                o = A(m, 192 + 32 * hf, 32)
-                mm(o, A("I32"), A("KW", 96 * par + 32 * h, 32), True, False)
                 for sg in (0, 1):
-                    mm(o, A("PB", 128 * (2 * hf + sg), 128), A("EL", 64 * h + sg, 32, 2), False, sg == 1)
-            if h in cfg["wf"]: cp(A("IX", 192 * h, 64), A(m, 192, 64))
-            for hf in (0, 1):
-                o = A(m, 256 + 32 * hf, 32)
-                for sg in (0, 1):
-                    mm(o, A("PM", 128 * (2 * hf + sg), 128), A(nm, 64 * h + sg, 32, 2), sg == 0, False)
-                for sg in (0, 1):
-                    mm(o, A("PK", 128 * (2 * hf + sg), 128), A("EL", 64 * h + sg, 32, 2), False, sg == 1)
+                    mm(A(m, 192 + 32 * hf, 32), A("PB", 128 * (2 * hf + sg), 128), A("EL", 64 * h + sg, 32, 2), False, hf + sg == 2)
+            mm(A(m, 256, 64), A("IB"), A("KA", 0, 64), True, False)
+            mm(A(m, 256, 64), A("IB"), A("KA", 64, 64), False, False)
             for li in (0, 1):
-                o = A(m, 320 + 32 * li, 32)
-                mm(o, A("I32"), A("KA", 48 * li, 32), True, False)
                 for sg in (0, 1):
-                    mm(o, A("WA", 128 * (2 * li + sg), 128), A("EL", 64 * h + sg, 32, 2), False, sg == 1)
-            o = 64 if h in cfg["wf"] else 0
-            cp(A("IX", 192 * h + o, 192 - o), A(m, 192 + o, 192 - o))
-            mark["w%d" % h] = act(A("WS%d" % h), IND(A("UW", 1472, 768), A("IX", 192 * h, 64)), "Copy")
-            tt(A("D%d" % h), IND(A(x), A("IX", 192 * h + 64, 64)), A("WS%d" % h), "sub")
-        sgn = A("SG%d" % par)
+                    mm(A(m, 256 + 32 * li, 32), A("WA", 128 * (2 * li + sg), 128), A("EL", 64 * h + sg, 32, 2), False, li + sg == 2)
+            cp(A("IX", 128 * h, 128), A(m, 192, 128))
+            win = A("UW", 1472 + 256 * h, 256) if t else A("U0B", 1280 + 256 * h, 256)
+            for c, n in (((0, 32), (32, 32)) if 2 - h in cfg["half"] else ((0, 64),)):
+                mark["w%d" % (2 - h)] = act(A("WS%d" % h, 16 * c, 16 * n), IND(win, A("IX", 128 * h + c, n)), "Copy")
+            for hf in (0, 1):
+                own = IND(A("UW", 192, 2048 + 384 * t) if t else A("U0B"), A("XL%d" % par, 96 * hf + 32 * h, 32))
+                tt(A("D%d" % h, 512 * hf, 512), own, A("WS%d" % h, 512 * hf, 512), "sub")
+        if not t:
+            for blk in range(3): turn_names(blk, mark["w0"])
+        if t and cfg["vg"] != "early": ghost_views(t, mark.get(cfg["vg"]))
+        if not last: names(t + 1)
+        ghost = A("GH%d" % par)
         mm(A("M0", 0, 192), A("IB"), A("EL"), True, False)
-        mm(A("M0", 0, 192), A("IH"), sgn, False, True)
+        mm(A("M0", 0, 192), A("IN1"), ghost, False, True)
         mm(A("M0", 192, 192), A("IN1"), A("EL"), True, False)
-        mm(A("M0", 192, 192), A("IH"), sgn, False, True)
-        act(A("FIT", 0, 192), A("M0", 0, 192), "Relu", -0.5)
-        act(A("FIT", 192, 192), A("M0", 192, 192), "Relu", 0.5)
+        mm(A("M0", 192, 192), A("IN1"), ghost, False, True)
+        act(A("FIT", 0, 192), A("M0", 0, 192), "Relu")
+        act(A("FIT", 192, 192), A("M0", 192, 192), "Relu", 1.0)
         for z in (0, 1):
             mm(A("M0", 192 * z, 192), A("MT"), A("FIT", 192 * z, 192), True, False)
-            mm(A("M0", 192 * z, 192), A("IK"), A("FIT", 192 * z, 192), False, False)
-            mm(A("M0", 192 * z, 192), A("I32"), A(nm), False, True)
+            mm(A("M0", 192 * z, 192), A("I16"), A(nm), False, True)
         act(A("VAL"), A("M0", 0, 384), "Relu", 192.0 - 2048.0)
         mm(A("M0", 0, 384), A("BO32"), A("VAL"))
         act(A("CAND"), A("M0", 0, 384), "Copy")
 
-        def scale(r):
-            if cfg["ss"]: act(r, r, "Copy", 0.0, 2.0 ** -6)
-            else: ts(r, r, 2.0 ** -6, "mul")
+        def summ(o, terms):
+            for k, a in enumerate(terms):
+                mm(o, A("I32"), a, k == 0, k == len(terms) - 1)
 
-        def shock(h, p):
-            d, q, bb = "D%d" % h, "QW%d" % h, "WS%d" % h
-            act(A(p), A(d), "Abs")
-            tt(A(q, 512, 1024), A(d), A(p), "mul")
-            lo, hi, o = A(q, 512, 512), A(q, 1024, 512), A(q, 1536, 512)
-            if h in cfg["pes"]:
-                mm(A(p, 0, 512), A("I32"), lo, True, False)
-                mm(A(p, 0, 512), A("I32"), hi, False, True)
-                if cfg["sv"]: cp(o, A(p, 0, 512))
-                else: act(o, A(p, 0, 512), "Copy")
+        def shock(k):
+            h = 2 - k
+            d, q, bb, how = "D%d" % h, "QW%d" % (h % 2), "WS%d" % h, cfg["pair"][k]
+            lo, hi, o, pa, pb = A(q, 512, 512), A(q, 1024, 512), A(q, 1536, 512), A("SA"), A("SB")
+            act(pa, A(d, 0, 512), "Abs")
+            tt(lo, A(d, 0, 512), pa, "mul")
+            act(pb, A(d, 512, 512), "Abs")
+            tt(pb if how == "s" else hi, A(d, 512, 512), pb, "mul")
+            if how == "s":
+                tt(o, lo, pb, "add")
+                act(hi, pb, "Copy")
+            elif how == "t":
+                summ(pa, [lo, hi])
+                act(o, pa, "Copy")
             else:
                 tt(o, lo, hi, "add")
-            mark["a%d" % h] = act(A(bb, 512, 512), IND(A(q), A("IX", 192 * h + 160, 32)), "Copy")
-            tt(A(bb, 0, 512), IND(A(q), A("IX", 192 * h + 128, 32)), A(bb, 512, 512), "add")
-            r = A(p, 512, 128)
-            if h in cfg["l3"]:
-                mm(r, A("I32"), A(bb, 0, 128, 4), True, False)
-                mm(r, A("I32"), A(bb, 2, 128, 4), False, True)
+            mark["g%d" % k] = act(A(bb, 512, 512), IND(A(q), A("IX", 128 * h + 96, 32)), "Copy")
+            tt(A(bb, 0, 512), IND(A(q), A("IX", 128 * h + 64, 32)), A(bb, 512, 512), "add")
+            r = A("SL", 128 * h, 128)
+            if k in cfg["c1"]:
+                summ(A("SL", 384, 128), [A(bb, 1, 128, 4), A(bb, 3, 128, 4)])
+                act(A(d, 0, 128), A("SL", 384, 128), "Copy")
             else:
-                tt(r, A(bb, 0, 128, 4), A(bb, 2, 128, 4), "add")
-            tt(A(d, 0, 128), A(bb, 1, 128, 4), A(bb, 3, 128, 4), "add")
-            tt(r, r, A(d, 0, 128), "add")
-            scale(r)
+                tt(A(d, 0, 128), A(bb, 1, 128, 4), A(bb, 3, 128, 4), "add")
+            summ(r, [A(bb, 0, 128, 4), A(bb, 2, 128, 4), A(d, 0, 128)])
+            act(r, r, "Copy", 0.0, 2.0 ** -6)
             for z in (0, 1):
-                w = A("UW", 1472 + 256 * h + 2 * par + z, 64, 4)
-                tt(w, w, A(p, 512 + z, 64, 2), "add")
+                tt(A("WN", 192 * z + 64 * h, 64), A("UW", 1472 + 256 * h + 2 * par + z, 64, 4), A("SL", 128 * h + z, 64, 2), "add")
 
-        def node(ci, p):
-            n, j0 = 64, 64 * ci
-            d, q, xg = "DA%d" % (ci % 2), "QS%d" % (ci % 2), 1024 * (ci % 3)
-            u = A("UC", j0, n)
-            xb = "EB" if t == 0 else "XG"
-            k = act(A(xb, xg, 1024), IND(A(x), A("TI", j0, n)), "Copy")
-            if ci in cfg["xg"] and cfg["xg"][ci] in mark: ops[k]["after"] = mark[cfg["xg"][ci]]
-            if t == 0 or ci in cfg["psub"]:
-                for k in range(16):
-                    mm(A(p, k * n, n), A("I32" if t else "IB"), A(xb, xg + k, n, 16), True, False)
-                    mm(A(p, k * n, n), A("I32" if t else "IB"), u if t else A("UB", j0, n), False, True)
-                act(A(d), A(p), "Abs")
+        def node(ch):
+            j0, n = CHUNK[ch]
+            q, c = take("qn", ("QN0", "QN1")), cfg["cb"] if ch == "c" else "NC"
+            u = A("UR", 4 * j0, 4 * n)
+            if not t:
+                for lo in range(0, n, 64):
+                    (cp if ch + str(lo // 64) in cfg["pe"][0] else lambda o, a: act(o, a, "Copy"))(A("XB", 16 * lo, 1024), IND(A(x), A(ti, j0 + lo, 64)))
+            for k in (0, 2, 1, 3):
+                p = A(take("bank", ("NA", "NB") if ch == "a" else ("NA", "NB", "SA", "SB")), 0, 4 * n)
+                d = A(take("nd", ("ND0", "ND1", "ND2")), 0, 4 * n)
+                xs = IND(A(x), A(ti, j0 + k * n // 4, n // 4))
+                if not t:
+                    for m in range(4):
+                        mm(A(p["b"], m * n, n), A("IB"), A("XB", 4 * k + m, n, 16), True, False)
+                        mm(A(p["b"], m * n, n), A("IN1"), A("U0B", 4 * j0, n, 4), False, True)
+                    act(d, p, "Abs")
+                elif "%s%d" % (ch, k) in cfg["pe"][t]:
+                    xg = A(take("xg", ("XG0", "XG1")), 0, 4 * n)
+                    act(xg, xs, "Copy")
+                    mm(p, A("I32"), xg, True, False)
+                    mm(p, A("N32"), u, False, True)
+                    act(d, p, "Abs")
+                else:
+                    tt(d, xs, u, "sub")
+                    act(p, d, "Abs")
+                if k == 2:
+                    tt(p, d, p, "mul")
+                    tt(A(q, 0, 4 * n), A(q, 0, 4 * n), p, "add")
+                elif k == 3 and ch in cfg["tree"][t]:
+                    c3 = p["b"]
+                    tt(A(c3, 0, 3 * n), A(d["b"], 0, 3 * n), A(c3, 0, 3 * n), "mul")
+                    tt(A(q, 11 * n, n), A(d["b"], 3 * n, n), A(c3, 3 * n, n), "mul")
+                else:
+                    tt(A(q, 4 * n * min(k, 2), 4 * n), d, p, "mul")
+            if ch in cfg["tree"][t]:
+                tt(A(c3, 0, 3 * n), A(c3, 0, 3 * n), A(q, 4 * n, 3 * n), "add")
+                tt(A(c3, 2 * n, n), A(c3, 2 * n, n), A(q, 2 * n, n), "add")
             else:
-                if cfg["us"]: act(A(p, 0, n), u, "Copy")
-                else: cp(A(p, 0, n), u)
-                for k in range(16):
-                    tt(A(d, k * n, n), A("XG", xg + k, n, 16), A(p, 0, n), "add")
-                act(A(p), A(d), "Abs")
-            tt(A(q, 0, 8 * n), A(d, 0, 8 * n), A(p, 0, 8 * n), "mul")
-            if cfg["pea"]:
-                o = 0
-                tt(A(q, 12 * n, 4 * n), A(d, 12 * n, 4 * n), A(p, 12 * n, 4 * n), "mul")
-                mm(A(p, 0, 4 * n), A("I32"), A(q, 4 * n, 4 * n), True, False)
-                mm(A(p, 0, 4 * n), A("I32"), A(q, 12 * n, 4 * n), False, True)
-                tt(A(p, 8 * n, 4 * n), A(p, 8 * n, 4 * n), A(d, 8 * n, 4 * n), "mul")
-            else:
-                o = 12 * n
-                tt(A(p, 8 * n, 8 * n), A(p, 8 * n, 8 * n), A(d, 8 * n, 8 * n), "mul")
-                tt(A(p, o, 4 * n), A(p, o, 4 * n), A(q, 4 * n, 4 * n), "add")
-            tt(A(q, 0, 4 * n), A(q, 0, 4 * n), A(p, 8 * n, 4 * n), "add")
-            tt(A(q, 0, 2 * n), A(q, 0, 2 * n), A(p, o, 2 * n), "add")
-            tt(A(p, o + 2 * n, 2 * n), A(p, o + 2 * n, 2 * n), A(q, 2 * n, 2 * n), "add")
-            tt(A(q, 0, n), A(q, 0, n), A(p, o + 2 * n, n), "add")
-            r = A(p, o + 3 * n, n)
-            tt(r, r, A(q, n, n), "add")
-            tt(r, r, A(q, 0, n), "add")
+                c3 = c
+                mm(A(c, 0, 3 * n), A("I32"), A(q, 4 * n, 3 * n), True, False)
+                mm(A(c, 0, 3 * n), A("I32"), A(q, 8 * n, 3 * n), False, False)
+                mm(A(c, 2 * n, n), A("I32"), A(q, 2 * n, n), False, True)
+            tt(A(q, 0, 2 * n), A(q, 0, 2 * n), A(c3, 0, 2 * n), "add")
+            tt(A(q, 0, n), A(q, 0, n), A(c3, 2 * n, n), "add")
+            r = A(c, 3 * n, n)
+            summ(r, [A(q, 7 * n, n), A(q, 11 * n, n), A(q, 3 * n, n), A(q, n, n), A(q, 0, n)])
             un = A("UW", 192 + t + 4 * j0, n, 4)
-            if ci < 2 or last: scale(r)
+            if ch == "a": act(r, r, "Copy", 0.0, 2.0 ** -6)
             else: tt(r, r, A("MK", j0 - 128, n), "mul")
             tt(un, un, r, "add")
 
-        done = []
+        def claims(lo, n):
+            w0, w1 = A("WN", lo, n), A("WN", 192 + lo, n)
+            if cfg["dd"] == "T":
+                dd = A("M1", 384, n)
+                mm(dd, A("I32"), w0, True, False)
+                mm(dd, A("N32"), w1, False, True)
+            else:
+                dd = A("DD", lo, n)
+                tt(dd, w0, w1, "sub")
+            ts(A("CMP", lo, n), dd, col("TH", 4), "gt", 0.59375, "sub")
+            ts(A("CMP", 192 + lo, n), dd, col("TH", 1), "lt", 0.59375, "sub")
+            for z in (0, 1):
+                mm(A("M1", 192 * z + lo, n), A("BOK"), A("CMP", 192 * z + lo, n))
+            tt(A("MM", lo, n), A("M1", lo, n), A("CAND", lo, n), "min")
+            tt(A("M1", 384, n), A("M1", 192 + lo, n), A("CAND", 192 + lo, n), "min")
+            tt(A("VV", lo, n), A("MM", lo, n), A("M1", 384, n), "max")
+            tt(A("PR", lo, n), A("VV", lo, n), A("DG", lo, n), "mul")
+            scan(A("S1", lo, n), A("KEEP", lo, n), A("PR", lo, n), 0.0, "mul", "add")
+            for c in range(lo // 16, (lo + n) // 16):
+                k, o = 192 - 16 * c, 8 * c * (25 - c)
+                ts(A("EQ", o, k), A("VV", 16 * c, k), col("S1", 16 * c + 15), "eq")
+                if k > 16: mm(A("M0", 16 * c + 16, k - 16), A("BOB"), A("EQ", o + 16, k - 16), False, False)
+                mm(A("M0", 16 * c, 16), A("BOI"), A("EQ", o, 16), False, lo == 0 and 16 * c + 16 == n)
 
-        def units(us):
-            for kind, ci in us:
-                (shock if kind == "s" else node)(int(ci), "P%d" % (turn[0] % 3))
-                turn[0] += 1
-                done.append(kind + ci)
-
-        units(cfg["lastA"] if last else cfg["A"])
-        if not last:
-            names(1 - par)
-        else:
-            dma("Y", ("ys", ALL), A("UW", 1472, 768), 4e5)
-        w0, w1 = A("UW", 1472 + 2 * par, 192, 4), A("UW", 1473 + 2 * par, 192, 4)
-        tt(A("DD"), w0, w1, "sub")
-        ts(A("CMP", 0, 192), A("DD"), col("TH", 4), "gt", 0.59375, "sub")
-        ts(A("CMP", 192, 192), A("DD"), col("TH", 1), "lt", 0.59375, "sub")
-        mm(A("M1", 0, 384), A("BOK"), A("CMP"))
-        tt(A("MM"), A("M1", 0, 384), A("CAND"), "min")
-        tt(A("VV"), A("MM", 0, 192), A("MM", 192, 192), "max")
-        tt(A("PR"), A("VV"), A("DG"), "mul")
-        scan(A("S1"), A("KEEP"), A("PR"), 0.0, "mul", "add")
-        o = 0
-        for c in range(12):
-            n = 192 - 16 * c
-            ts(A("EQ", o, n), A("VV", 16 * c, n), col("S1", 16 * c + 15), "eq", col("WT", 16 * c + 15), "mul")
-            mm(A("M0", 16 * c, n), A("BOB"), A("EQ", o, n), c == 0, c == 11)
-            o += n
-        tt(A("MW", 0, 192), A("M1", 0, 192), w0, "min")
-        tt(A("MW", 192, 192), A("M1", 192, 192), w1, "min")
-        ts(A("DN", 0, 192), A("M1", 192, 192), 0.0, "gt", 1664.0, "mul")
-        act(A("DN", 192, 192), A("DN", 0, 192), "Sign")
-        tt(A("M0", 0, 192), A("M0", 0, 192), A("THR"), "lt")
-        tt(A("PR"), A("M0", 0, 192), A("VV"), "mul")
+        mm(A("M0", 0, 192), A("IB"), A("THR"), True, False)
+        for k in range(3):
+            shock(k)
+            if k == 0 and cfg["cl"] == 3: claims(128, 64)
+            if k == 1: claims(*((64, 64) if cfg["cl"] == 3 else (64, 128)))
+        claims(0, 64)
+        for c0, c1 in cfg["vr"]: views(t, c0, c1, "r" in cfg["vv"][t], mark.get(cfg["vra"]))
+        node("a")
+        for z in (0, 1):
+            gcp(A("UW", 1472 + 2 * par + z, 192, 4), A("WN", 192 * z, 192))
+        if last: dma("Y", ("ys", ALL), A("UW", 1472, 768), 128, 3072)
+        tt(A("MW"), A("M1", 0, 384), A("WN"), "min")
+        act(A("DN"), A("M1", 192, 192), "Sign")
+        tt(A("PR"), A("M0", 0, 192), A("VV"), "min")
         scan(A("S2"), A("TD"), A("PR"), 1e6, "min", "max")
         pos, pu = A("S2", 15, 12, 16), A("PU")
         cp(pu, pos)
         if not last:
-            cp(IND(A("SD%d" % (t + 1), 0, 1472), pu), A("DN", 0, 192))
+            cp(IND(A("SD%d" % (t + 1), 0, 1472), pu), A("DN"))
             send_sides(t + 1)
-        tt(IND(A("C"), pu), A("DN", 192, 192), A("W2S", par, 192, 2), "add")
+        tt(IND(A("C"), pu), A("DN"), A("W2S", par, 192, 2), "mul")
         hl, ha = A("HL", 12 * par, 12), A("HA", 0, 12)
         ts(ha, pos, 192.0, "lt", 4096.0, "mul")
         tt(ha, ha, hl, "min")
@@ -455,34 +541,36 @@ def build_ops(cfg):
             ts(A("HU", 12 * par, 12), hl, -192.0, "add")
         else:
             host_out(par)
-        if not last:
-            view_lists(0, 80)
-        else:
-            dma("Y", ("yc", ALL), {"b": "C", "lo": 192, "n": 1280, "st": 1, "p": (0, 128, 16)}, 4e4)
+        if last:
+            for b in range(16):
+                mm(A("M1", 384, 80), A("D32", 128 * b, 128), A("C", 192 + 80 * b, 80), b == 0, b == 15)
+            ts(A("VA", 0, 80), A("M1", 384, 80), -1280.0, "add")
+            ts(A("VA", 80, 80), A("M1", 384, 80), -1.0, "mul", -1281.0, "add")
+            tt(A("VA", 0, 80), A("VA", 0, 80), A("VA", 80, 80), "max")
+            dma("Y", ("yc", ALL), A("VA", 0, 80), 128, 320)
             for gq in range(8):
-                dma("YS"[gq % 2], ("yh", (gq, slice(None))), A("YH", 32 * gq, 32, p=(0, 12)), 2e3)
-        units([k for k in ("n0", "n1") if k not in done])
+                dma("Y", ("yh", (gq, slice(None))), A("YH", 32 * gq, 32, p=(0, 12)), 12, 128)
+        tt(IND(A("UW", 0, 1472), pu), A("MW", 0, 192), A("MW", 192, 192), "max")
         if not last:
-            tt(IND(A("UW", 0, 1472), pu), A("MW", 0, 192), A("MW", 192, 192), "max")
-            views(t + 1, 0, 24, "g" in cfg["vv"])
-            send_views(t + 1)
-            mm(A("M0", 0, 192), A("IB"), A("SD%d" % (t + 1), 192 + t + 512, 192, 4), True, False)
-            mm(A("M0", 0, 192), A("IN1"), A(sd, 192 + t + 512, 192, 4), False, True)
-            act(A("MK"), A("M0", 0, 192), "Abs")
-            act(A("MK"), A("MK"), "Relu", col("TH", 3), -1.0)
-            for k, c0, c1 in (("n2", 24, 48), ("n3", 48, 64), ("n4", 64, 80)):
-                units([k])
-                views(t + 1, c0, c1, k in cfg["vv"])
+            send_values(t + 1)
+            if cfg["vg"] == "early": ghost_views(t + 1)
+            new = A("SD%d" % (t + 1), 192 + t + 512, 192, 4)
         else:
-            units([k for k in ("n2", "n3", "n4") if k not in done])
-            tt(IND(A("UW", 0, 1472), pu), A("MW", 0, 192), A("MW", 192, 192), "max")
-            dma("Y", ("yu", (slice(None), slice(0, 640))), A("UW", 192, 640), 3.3e5)
-            dma("S", ("yu", (slice(None), slice(640, 1280))), A("UW", 832, 640), 3.3e5)
+            dma("Y", ("yu", (slice(None), slice(0, 512))), A("UW", 192, 512), 128, 2048)
+            new = A("SN")
+            act(new, A("C", 192 + t + 512, 192, 4), "Sign")
+        mm(A("M0", 0, 192), A("IB"), new, True, False)
+        mm(A("M0", 0, 192), A("IB"), A(sd, 192 + t + 512, 192, 4), False, True)
+        act(A("MK"), A("M0", 0, 192), "Abs", 0.0, 2.0 ** -7)
+        for ch in "bc":
+            node(ch)
+            j0, n = CHUNK[ch]
+            if last: dma("Y", ("yu", (slice(None), slice(4 * j0, 4 * (j0 + n)))), A("UW", 192 + 4 * j0, 4 * n), 128, 16 * n)
     return ops
 
 
 ASYNC = ("dma", "rem", "arr")
-HOP = 0.1
+HOP, ROW, RATE = 0.1, 0.08, 2e4
 
 
 def plan(cfg):
@@ -503,6 +591,7 @@ def plan(cfg):
             for s2, j, w2 in hist.get(b, ()):
                 if w2 and ops[j]["k"] == "mm" and s2[1] // 512 == lo // 512 and j not in dep: dep[j] = False
         if "after" in o: dep.setdefault(o["after"], False)
+        if "behind" in o: dep[o["behind"]] = True
         o["dep"] = dep
         for acc, w in ((o["rd"], False), (o["wr"], True)):
             for s in acc:
@@ -511,71 +600,131 @@ def plan(cfg):
                     h[:] = [r for r in h if not (s[1] <= r[0][1] and r[0][2] <= s[2] and dep.get(r[1]))]
                 h.append((s, i, w))
     n = len(ops)
-    pri = [0.0] * n
-    for i in range(n - 1, -1, -1):
-        pri[i] += ops[i]["cost"] + ops[i]["lat"]
-        for j in ops[i]["dep"]:
-            pri[j] = max(pri[j], pri[i] + HOP)
-    r = cfg["seed"]
-    for i in range(n):
-        r = (r * 1103515245 + 12345) % 2147483648
-        pri[i] += cfg["noise"] * r / 2147483648
     pred, succ = [[] for _ in range(n)], [[] for _ in range(n)]
+    anc = [0] * n
     for i, o in enumerate(ops):
+        for j in o["dep"]: anc[i] |= anc[j]
+        far = anc[i]
         for j, hard in o["dep"].items():
+            anc[i] |= 1 << j
+            if far >> j & 1 and not ops[j]["lat"]: continue
             d = ops[j]["lat"] + HOP if (hard or o["k"] == "arr") else 0.0
             pred[i].append((j, d))
             succ[j].append((i, d))
     cost, eng = [o["cost"] + 1e-6 for o in ops], [o["e"] for o in ops]
 
-    def place(seq, before, rel):
-        st = [0.0] * n
-        busy = {e: [] for e in "VSTGYR"}
+    rnd = [cfg["seed"]]
+
+    def draw():
+        rnd[0] = (rnd[0] * 1103515245 + 12345) % 2147483648
+        return (rnd[0] + 0.5) / 2147483648
+
+    def place(seq, before, rel, free):
+        st, busy = {}, {e: [(-1.0, free[e])] for e in free}
         for i in seq:
-            s = rel[i]
+            s, c = rel[i], cost[i]
             for j, d in before[i]:
-                x = st[j] + cost[j] + d
+                x = st[j] + d
                 if x > s: s = x
             b = busy[eng[i]]
-            lo, hi = 0, len(b)
-            while lo < hi:
-                m = (lo + hi) // 2
-                if b[m][1] <= s: lo = m + 1
-                else: hi = m
-            while lo < len(b) and b[lo][0] < s + cost[i]:
-                s = b[lo][1]
-                lo += 1
-            b.insert(lo, (s, s + cost[i]))
+            lo = len(b)
+            if b[-1][1] > s:
+                lo, hi = 0, lo - 1
+                while lo < hi:
+                    m = (lo + hi) // 2
+                    if b[m][1] <= s: lo = m + 1
+                    else: hi = m
+                while lo < len(b) and b[lo][0] < s + c:
+                    s = b[lo][1]
+                    lo += 1
+            b.insert(lo, (s, s + c))
             st[i] = s
-        return st
+        return st, busy
 
-    zero, lats = [0.0] * n, [o["lat"] for o in ops]
+    def improve(calls, key, head, tail, free, after, steps, heat):
+        mine = set(calls)
+        pre = {i: [(j, cost[j] + d) for j, d in pred[i] if j in mine] for i in calls}
+        suc = {i: [(j, cost[j] + d) for j, d in succ[i] if j in mine] for i in calls}
+
+        def span_of(st, busy):
+            i = max(calls, key=lambda i: st[i] + cost[i] + tail[i])
+            end = st[i] + cost[i] + tail[i]
+            for e, b in busy.items():
+                if len(b) > 1 and b[-1][1] + after[e] > end: end, i = b[-1][1] + after[e], e
+            return end, st, i
+
+        def both(st):
+            back = place(sorted(calls, key=lambda i: -st[i] - cost[i]), suc, tail, after)[0]
+            return place(sorted(calls, key=lambda i: -back[i] - cost[i]), pre, head, free)
+
+        now = best = span_of(*place(sorted(calls, key=lambda i: key[i]), pre, head, free))
+        pairs = None
+        for it in range(steps):
+            if pairs is None:
+                iss, prev, lastq, pairs = now[1], {}, {}, []
+                for i in sorted(calls, key=lambda i: iss[i]):
+                    prev[i] = lastq.get(eng[i])
+                    lastq[eng[i]] = i
+                i = lastq.get(now[2], now[2])
+                while i is not None:
+                    s, k = head[i], None
+                    for j, d in pre[i]:
+                        if iss[j] + d > s: s, k = iss[j] + d, j
+                    if s < iss[i] - 1e-7:
+                        k = prev[i]
+                        if k is not None: pairs.append((k, i))
+                    i = k
+            if not pairs: break
+            key = dict(now[1])
+            p, i = pairs[int(draw() * len(pairs))]
+            if draw() < 0.5:
+                while draw() < 0.5 and prev[p] is not None: p = prev[p]
+                key[i] = key[p] - 1e-4
+                todo = [i]
+                while todo:
+                    k = todo.pop()
+                    for j, d in pre[k]:
+                        if key[j] >= key[k]:
+                            key[j] = key[k] - 1e-7
+                            todo.append(j)
+            else:
+                key[p] = key[i] + 1e-4 + (draw() < 0.3) * 2 * draw()
+                todo = [p]
+                while todo:
+                    k = todo.pop()
+                    for j, d in suc[k]:
+                        if key[j] <= key[k]:
+                            key[j] = key[k] + 1e-7
+                            todo.append(j)
+            got = place(sorted(calls, key=lambda i: key[i]), pre, head, free)
+            got = span_of(*(both(got[0]) if it % cfg["fbe"] == 0 else got))
+            if got[0] <= now[0] - heat * (1 - it / steps) * math.log(draw()): now, pairs = got, None
+            if got[0] < best[0]: best = got
+        return best
+
+    zero, lats, idle, every = [0.0] * n, [o["lat"] for o in ops], {e: 0.0 for e in "VSTGYR"}, list(range(n))
     top = [0.0] * n
     for i in range(n - 1, -1, -1):
-        top[i] = max([pri[i]] + [top[k] + 1e-9 for k, d in succ[i]])
-    seq = sorted(range(n), key=lambda i: -top[i])
-    best = None
-    for it in range(cfg["fb"]):
-        iss = place(seq, pred, zero)
-        end = max(iss[i] + cost[i] + lats[i] for i in range(n))
-        if best is None or end < best[0]: best = (end, iss)
-        back = place(sorted(range(n), key=lambda i: -(iss[i] + cost[i])), succ, lats)
-        seq = sorted(range(n), key=lambda i: -(back[i] + cost[i]))
+        top[i] = cost[i] + max([lats[i]] + [top[k] + d + 1e-9 for k, d in succ[i]])
+    best = improve(every, [-x for x in top], zero, lats, idle, idle, cfg["all"], cfg["heat"])
+    allsuc = {i: [(j, cost[j] + d) for j, d in succ[i]] for i in every}
+    t0 = 0.0
     for it in range(cfg["ls"]):
-        key = list(best[1])
-        r = (r * 1103515245 + 12345) % 2147483648
-        t0, amp = best[0] * r / 2147483648, (0.5, 1.5, 3.0)[it % 3]
-        for i in range(n):
-            if t0 - 8 < key[i] < t0 + 8:
-                r = (r * 1103515245 + 12345) % 2147483648
-                key[i] += amp * (r / 2147483648 - 0.5)
-            for j, d in pred[i]:
-                if key[j] >= key[i]: key[i] = key[j] + 1e-7
-        iss = place(sorted(range(n), key=lambda i: key[i]), pred, zero)
-        back = place(sorted(range(n), key=lambda i: -(iss[i] + cost[i])), succ, lats)
-        iss = place(sorted(range(n), key=lambda i: -(back[i] + cost[i])), pred, zero)
-        end = max(iss[i] + cost[i] + lats[i] for i in range(n))
-        if end <= best[0]: best = (end, iss)
+        iss, t1 = best[1], t0 + cfg["wide"]
+        back = place(sorted(every, key=lambda i: -iss[i] - cost[i]), allsuc, lats, idle)[0]
+        calls = [i for i in every if t0 <= iss[i] < t1]
+        head, tail, free, after = {}, {}, dict(idle), dict(idle)
+        for i in every:
+            if iss[i] < t0: free[eng[i]] = max(free[eng[i]], iss[i] + cost[i])
+            elif iss[i] >= t1: after[eng[i]] = max(after[eng[i]], back[i] + cost[i])
+        for i in calls:
+            head[i] = max([0.0] + [iss[j] + cost[j] + d for j, d in pred[i] if iss[j] < t0])
+            tail[i] = max([lats[i]] + [back[j] + cost[j] + d for j, d in succ[i] if iss[j] >= t1])
+        st = improve(calls, iss, head, tail, free, after, cfg["steps"], cfg["heat"])[1]
+        key = [st[i] if i in st else iss[i] if iss[i] < t0 else 1e4 - back[i] - cost[i] for i in every]
+        got = improve(every, key, zero, lats, idle, idle, 0, 0)
+        if got[0] <= best[0] + cfg["slack"]: best = got
+        t0 = t0 + cfg["wide"] * (0.2 + 0.3 * draw()) if t1 < best[0] else 0.0
     iss = best[1]
     fin = [iss[i] + cost[i] + lats[i] for i in range(n)]
     order = sorted(range(n), key=lambda i: iss[i])
@@ -605,13 +754,13 @@ def plan(cfg):
             o["id"], o["clock"] = ("d%d" % nd, 1), dict(kn)
             nd += 1
         else:
-            cnt[o["e"]] += 1
+            cnt[o["e"]] += len(o["a"]) if o["k"] == "mm" else 1
             o["id"], o["clock"] = ("c" + o["e"], cnt[o["e"]]), dict(kn)
     return ops, order, cnt, nd, iss, fin
 
 
 OPS, ORDER, CNT, NDMA, ISS, FIN = plan(CFG)
-SEMAPHORES = ["cV", "cS", "cT", "cG"] + ["d%d" % k for k in range(NDMA)] + ["as%d" % t for t in range(RO)] + ["av%d" % t for t in range(RO)]
+SEMAPHORES = ["cV", "cS", "cT", "cG"] + ["d%d" % k for k in range(NDMA)] + [k + str(t) for k in ("as", "ao", "av") for t in range(RO)]
 ALU = {"add": AluOpType.add, "sub": AluOpType.subtract, "mul": AluOpType.mult, "max": AluOpType.max, "min": AluOpType.min,
        "ge": AluOpType.is_ge, "gt": AluOpType.is_gt, "lt": AluOpType.is_lt, "eq": AluOpType.is_equal,
        "and": AluOpType.bitwise_and, "shr": AluOpType.arith_shift_right}
@@ -662,15 +811,18 @@ def rank_program(g, core, T, topo):
         if k == "dma":
             q.dma_start(ap(a[0]), ap(a[1])).then_inc(sem, 16)
             continue
+        if k == "mm":
+            for m in a: q.matmul(ap(m[0]), ap(m[1]), ap(m[2]), m[3], m[4]).then_inc(sem, 1)
+            continue
         if k == "tt": r = q.tensor_tensor(ap(a[0]), ap(a[1]), ap(a[2]), ALU[a[3]])
         elif k == "ts":
             if a[5] is None: r = q.tensor_scalar(ap(a[0]), ap(a[1]), ap(a[2]), None, ALU[a[4]])
             else: r = q.tensor_scalar(ap(a[0]), ap(a[1]), ap(a[2]), ap(a[3]), ALU[a[4]], ALU[a[5]])
         elif k == "cp": r = q.tensor_copy(ap(a[0]), ap(a[1]))
+        elif k == "gcp": r = q.affine_select(ap(a[0]), ap(a[1]), [[1, a[0]["n"]]], ALU["ge"], 0.0, 0, 0)
         elif k == "ms": r = q.memset(ap(a[0]), a[1])
         elif k == "scan": r = q.tensor_tensor_scan(ap(a[0]), ap(a[1]), ap(a[2]), a[3], ALU[a[4]], ALU[a[5]])
         elif k == "act": r = q.activation(ap(a[0]), ap(a[1]), FUN[a[2]], bias=ap(a[3]), scale=ap(a[4]))
-        elif k == "mm": r = q.matmul(ap(a[0]), ap(a[1]), ap(a[2]), a[3], a[4])
         elif BUF[a[0]["b"]][1] == I: r = q.iota(ap(a[0]), a[1], a[2], a[3])
         else: r = q.iota(ap(a[0]), a[1], a[2], a[3], allow_small_or_imprecise_dtypes=True)
         r.then_inc(sem, 1)

import math
from concourse.bass import DstId, RemoteDMATransfer
from concourse.mybir import AluOpType, ActivationFunctionType

CFG = {"vg": "early", "vra": None, "cl": 3, "pair": "svs", "c1": (), "one": True, "cb": "SL", "vr": ((24, 52), (52, 80)),
       "half": (0, 1, 2), "ev": ((1,), (1,), (1,), (1,)), "dd": "T", "vv": ("r", "", "", ""),
       "pe": ("a0", "a1 a3 b0 b2", "a1 a3 b0 b2", "a1 a3 b0 b2 b1"), "tree": ("abc", "abc", "abc", "abc"), "rot": "Y",
       "run": 0.9, "fbe": 5, "heat": 0.15, "all": 100, "ls": 170, "wide": 16, "steps": 300, "slack": 0.0, "seed": 0}
RO = 4
F, B, H, I, U = "float32", "bfloat16", "float16", "int32", "uint16"
BUF = {
    "UW": (3392, F), "C": (1472, F), "TL": (1280, I), "IN": (1280, I), "U0B": (2432, B), "XC": (1280, H), "TH": (8, F),
    "WN": (384, F), "XL0": (384, U), "XL1": (384, U), "SO": (384, F), "SOB": (384, B),
    "D0": (1024, F), "D1": (1024, F), "D2": (1024, F), "WS0": (1024, F), "WS1": (1024, F), "WS2": (1024, F),
    "QW0": (2048, F), "QW1": (2048, F), "R32": (128, F),
    "ND0": (512, F), "ND1": (512, F), "ND2": (512, F), "QN0": (1536, F), "QN1": (1536, F), "XG0": (512, F), "XG1": (512, F),
    "XB": (2048, B), "UR": (1280, F), "IQ": (128, B), "TS": (1536, H), "REP": (320, B), "SLT": (128, B), "T3": (320, F),
    "PM": (512, H), "PB": (512, B), "PK": (512, B), "KW": (128, B), "KA": (128, B),
    "EB": (3072, B), "EL": (192, B), "IX": (384, U), "NM0": (192, H), "NM1": (192, H),
    "GH0": (192, B), "GH1": (192, B), "FIT": (384, B), "VAL": (384, F), "CAND": (384, F),
    "TI0": (320, U), "TI1": (320, U), "TF": (1280, H), "MK": (192, F), "SN": (192, B), "HL": (24, F), "HU": (24, U), "HA": (24, F), "YH": (256, F),
    "DD": (192, F), "CMP": (384, B), "MM": (384, F), "VV": (192, H), "PR": (192, F), "S1": (192, F), "S2": (192, F),
    "EQ": (1248, B), "PU": (12, U), "MW": (384, F), "DN": (192, F),
    "VA": (160, F), "VL": (160, U), "ST": (384, B), "SV": (384, F), "SVB": (384, B),
    "IK": (128, B), "JF": (192, F), "JG": (128, F), "PI": (8, I), "PF": (20, F), "OH": (16, F), "T1": (192, F), "T2": (192, F), "TJ": (192, F),
    "I32": (128, F), "N32": (128, F), "IB": (128, B), "I16": (128, H), "IN1": (128, B), "ROT": (128, B),
    "BO32": (128, F), "BOB": (128, B), "BOK": (128, B), "MT": (128, B), "WA": (512, B), "RR": (384, H),
    "D32": (2048, F), "DB": (2048, B), "DG": (192, F), "KEEP": (192, F), "TD": (192, F), "THR": (192, B), "BOI": (128, B),
    "W2S": (384, F), "ML": (160, F),
}
for _t in range(RO):
    BUF["X%d" % _t] = (3328, F if _t else B)
    BUF["SD%d" % _t] = (1856, B)
PS = {"SA": 512, "SB": 512, "SL": 512, "NA": 512, "NB": 512, "NC": 512, "M0": 512, "M1": 512}
ALIAS = {"VAL": "MM", "JG": "WN", "TJ": "DN", "T1": "MK", "T2": "CAND", "JF": "SO", "YH": "X1", "VV": "RR", "SN": "ST", "T3": "ND0", "SVB": "FIT", "SOB": "CMP", "DD": "S2"}
CHUNK = {"a": (0, 128), "b": (128, 128), "c": (256, 64)}
SCRATCH = {k: ("sbuf", [128, v[0]], v[1]) for k, v in BUF.items() if k not in ALIAS}
for _k, _v in PS.items():
    SCRATCH[_k] = ("psum", [128, _v], F)


def A(name, lo=0, n=None, step=1, p=(0, 128)):
    if n is None:
        n = (BUF[name][0] if name in BUF else PS[name]) - lo
    return {"b": ALIAS.get(name, name), "lo": lo, "n": n, "st": step, "p": p}


def IND(win, off):
    return {"b": win["b"], "lo": win["lo"], "n": 16 * off["n"], "st": 1, "p": (0, 128), "wn": win["n"], "off": off}


def isap(x):
    return isinstance(x, dict)


def span(a):
    return (a["b"], a["lo"], a["lo"] + (a["wn"] if "off" in a else (a["n"] - 1) * a["st"] + 1), a["st"], a["p"])


def meet(a, b):
    if a[1] >= b[2] or b[1] >= a[2] or a[4][0] >= b[4][1] or b[4][0] >= a[4][1]: return False
    return (a[1] - b[1]) % math.gcd(a[3], b[3]) == 0


def build_ops(cfg):
    ops = []

    def add(e, kind, outs, ins, cost, **kw):
        rd, wr = [], []
        for a in outs:
            wr.append(span(a))
            if "off" in a: rd.append(span(a["off"]))
        for a in ins:
            if isap(a):
                rd.append(span(a))
                if "off" in a: rd.append(span(a["off"]))
        d = {"e": e, "k": kind, "rd": rd, "wr": wr, "cost": cost, "lat": 0.0}
        d.update(kw)
        ops.append(d)
        return len(ops) - 1

    def vc(out, i0, c):
        n = out["n"]
        if "off" in out: return 0.05 + n * 3.8 * 0.00083
        if "off" in i0: return 0.05 + n * 1.56 * 0.00083
        return 0.02 + max(64, n * c) * 0.00083

    def two(*a):
        return all(x["b"] in BUF and BUF[x["b"]][1] in (B, H, U) for x in a)

    def tt(o, a, b, op):
        c = 1 if (a["b"] in PS or b["b"] in PS) else 2
        return add("V", "tt", [o], [a, b], vc(o, a, c), a=(o, a, b, op))

    def ts(o, a, s1, op0, s2=None, op1=None):
        return add("V", "ts", [o], [a, s1, s2], vc(o, a, 0.5 if two(o, a) else 1), a=(o, a, s1, s2, op0, op1))

    def cp(o, a):
        return add("V", "cp", [o], [a], vc(o, a, 0.5 if two(o, a) else 1), a=(o, a))

    def ms(o, v):
        return add("V", "ms", [o], [], vc(o, o, 1), a=(o, v))

    def scan(o, d0, d1, init, op0, op1):
        return add("V", "scan", [o], [d0, d1], vc(o, d0, 1), a=(o, d0, d1, init, op0, op1))

    def act(o, a, f, bias=0.0, scale=1.0):
        return add("S", "act", [o], [a, bias, scale], vc(o, a, 1) + 0.02, a=(o, a, f, bias, scale))

    def mm(o, l, r, start=True, stop=True):
        w = 4 if BUF[r["b"]][1] == F else 1
        k = add("T", "mm", [o], [l, r] + ([] if start else [o]), 0.01 + max(64, r["n"]) * w * 0.00042, a=[(o, l, r, start, stop)], acc=not start)
        a, b = ops[k - 1], ops[k]
        if not start and a["k"] == "mm" and a["cost"] + b["cost"] < cfg["run"]:
            for f in ("rd", "wr", "a", "cost"): a[f] += b[f]
            a["rd"] = [s for s in a["rd"] if a["acc"] or s[0] != o["b"]]
            ops.pop()

    def iota(o, pat, base, cm):
        return add("G", "iota", [o], [], 0.13 + o["n"] * 2 * 0.00083, a=(o, pat, base, cm))

    def gcp(o, a):
        return add("G", "gcp", [o], [a], 0.17 + o["n"] * 2 * 0.00083, a=(o, a))

    def dma(q, o, a, rows, nbytes):
        move = max(1, rows / 16) * (ROW + nbytes / RATE)
        if q == "Y": return add(q, "dma", [o] if isap(o) else [], [a], max(0.1, move), a=(o, a), lat=1.8)
        return add(q, "dma", [o] if isap(o) else [], [a], 1.0 if q == "G" else 0.1, a=(o, a), lat=1.8 + move)

    def send(sem, tr):
        size = 4 if BUF[tr[0][0]["b"]][1] == F else 2
        s = add("G", "rem", [], [b for a, b in tr], 1.0, tr=tr, sem=sem, lat=0.8 + 16 * len(tr) * (ROW + tr[0][0]["n"] * size / RATE))
        add("R", "arr", [a for a, b in tr], [], 0.0, sem=sem, ntr=len(tr), after=s, lat=0.8)
        return s

    def col(name, c):
        return A(name, c, 1)

    ALL = (slice(None), slice(None))
    dma("Y", A("IN", 0, 1280, p=(0, 8)), ("sd", ALL), 16, 2560)
    dma("Y", A("IN", 0, 1280, p=(8, 16)), ("nr", ALL), 16, 2560)
    dma("Y", A("IN", 0, 384, p=(16, 24)), ("hs", ALL), 16, 768)
    dma("S", A("U0B", 0, 1280), ("u0", ALL), 128, 2560)
    dma("S", A("U0B", 1280, 768), ("w0", ALL), 256, 1536)
    dma("Y", A("TL"), ("tl", ALL), 128, 5120)
    dma("Y", col("TH", 4), ("th", ALL), 128, 4)
    iota(col("PI", 0), [[0, 1]], 0, 1)
    iota(A("JF"), [[1, 192]], 0, 0)
    iota(A("JG"), [[1, 8], [0, 16]], 0, 0)
    iota(A("TJ"), [[0, 12], [1, 16]], 0, 0)
    iota(A("W2S"), [[2, 384]], 1281, 0)
    cp(col("PF", 0), col("PI", 0))
    for c, (s, op) in enumerate(((15, "and"), (4, "shr"), (7, "and"), (3, "shr"))):
        ts(col("PI", 1 + c), col("PI", 0), s, op)
    cp(A("PF", 1, 4), A("PI", 1, 4))
    ts(col("PF", 4), col("PF", 4), 1.0, "add")
    ts(col("PF", 5), col("PF", 0), 16.0, "ge")
    ts(col("PF", 16), col("PF", 4), 2.0, "eq", 2.0, "mul")
    ts(col("PF", 18), col("PF", 4), 1.0, "eq", -0.5, "mul")
    ts(col("PF", 17), col("PF", 16), 640.5 / 2, "mul", col("PF", 18), "add")
    ts(A("RR", 0, 128), A("JG"), col("PF", 3), "eq", col("PF", 16), "mul")
    ts(A("RR", 128, 128), A("JG"), col("PF", 3), "eq", 2.0, "mul")
    ts(A("RR", 256, 128), A("JG"), col("PF", 3), "eq", col("PF", 5), "mul")
    ts(A("I32"), A("JF", 0, 128), col("PF", 0), "eq")
    ts(A("OH"), A("JF", 0, 16), col("PF", 1), "eq")
    for b in range(16):
        act(A("D32", 128 * b, 128), A("I32"), "Copy", 0.0, col("OH", b))
    act(A("IB"), A("I32"), "Copy")
    act(A("R32", 0, 112), A("I32", 16, 112), "Copy")
    act(A("R32", 112, 16), A("I32", 0, 16), "Copy")
    act(A("ROT"), A("R32"), "Copy")
    ts(A("ML", 80, 80), A("JF", 0, 80), 16.0, "mul", col("PF", 1), "add")
    ts(A("ML", 0, 80), A("ML", 80, 80), 1.0, "add")
    ts(A("ML", 80, 80), A("ML", 80, 80), -1.0, "mul")
    ts(A("DG"), A("TJ"), col("PF", 1), "eq")
    act(A("KEEP"), A("TJ"), "Sign")
    for b in range(16):
        ts(A("DB", 128 * b, 128), A("IB"), col("OH", b), "mul")
    cp(A("I16"), A("IB"))
    act(A("IN1"), A("I32"), "Copy", 0.0, -1.0)
    act(A("N32"), A("I32"), "Copy", 0.0, -1.0)
    act(A("IQ"), A("I32"), "Copy", 0.0, 0.25)
    for c0, w in ((0, 8), (8, 8), (16, 4)):
        iota(A("T3", 16 * c0, 16 * w), [[0, 16], [1, w]], c0, 0)
    ts(A("REP"), A("T3"), col("PF", 0), "eq", 0.25, "mul")
    act(A("IK"), A("I32"), "Copy", 0.0, 2048.0)
    ts(A("BO32"), A("JG"), col("PF", 2), "eq")
    act(A("BOB"), A("BO32"), "Copy", 0.0, -2.0 ** 46)
    act(A("BOK"), A("BO32"), "Copy", 0.0, 4096.0)
    ts(A("T1", 0, 128), A("JF", 0, 128), col("PF", 0), "gt", -2048.0, "mul")
    tt(A("T1", 0, 128), A("T1", 0, 128), A("BO32"), "mul")
    tt(A("MT"), A("T1", 0, 128), A("IK"), "add")
    ts(col("TH", 1), col("TH", 4), -1.0, "mul")
    ts(col("PF", 7), col("PF", 1), 8.0, "ge", 512.0, "mul")
    ts(col("PF", 7), col("PF", 7), 512.0, "add")
    ts(col("PI", 5), col("PI", 0), 3, "and")
    ts(col("PI", 6), col("PI", 0), 2, "shr", 1, "and")
    ts(col("PI", 7), col("PI", 0), 3, "shr", 1, "and")
    cp(A("PF", 8, 3), A("PI", 5, 3))
    ts(col("PF", 11), col("PF", 10), -1.0, "mul", 1.0, "add")
    ts(col("PF", 12), col("PF", 10), -8.0, "mul", col("PF", 0), "add")
    ts(col("PF", 13), col("PF", 10), 4.0, "mul")
    ts(A("S1", 0, 144), A("JF", 0, 144), -16.0, "add", col("PF", 12), "eq")
    ts(col("PF", 15), col("PF", 2), 16.0, "mul", col("PF", 8), "add")
    ts(A("S2", 0, 144), A("JF", 0, 144), -16.0, "add", col("PF", 15), "eq")
    tt(A("PR", 4, 140), A("S2", 0, 140), A("S2", 4, 140), "sub")
    tt(col("PF", 6), col("PF", 7), col("PF", 9), "mul")
    tt(col("PF", 7), col("PF", 7), col("PF", 6), "sub")
    for hf in (0, 1):
        for sg in (0, 1):
            act(A("PB", 128 * (2 * hf + sg), 128), A("S1", 16 - 8 * sg, 128), "Copy", 0.0, col("PF", 11 - hf))
            act(A("WA", 128 * (2 * hf + sg), 128), A("PR", 16 - 8 * sg, 128), "Copy", 0.0, col("PF", 7 - hf))
    cp(A("PM"), A("PB"))
    act(A("PK"), A("PB"), "Copy", 0.0, 384.0)
    iota(A("SV", 0, 128), [[2, 2], [0, 2], [8, 32]], 0, 0)
    iota(A("SV", 128, 64), [[0, 2], [16, 32]], 0, 0)
    iota(A("SV", 192, 64), [[4, 2], [0, 32]], 0, 0)
    ts(A("KW"), A("SV", 0, 128), col("PF", 13), "add")
    ts(col("PF", 9), col("PF", 9), -1536.0, "mul", 1536.0, "add")
    ts(col("PF", 14), col("PF", 10), 8.0, "mul", col("PF", 8), "add")
    ts(A("KA", 0, 64), A("SV", 128, 64), col("PF", 9), "add")
    ts(A("KA", 64, 64), A("SV", 192, 64), col("PF", 14), "add")
    ms(A("HA", 0, 16), 0.5)
    scan(A("VA", 0, 16), A("HA", 0, 16), A("OH"), 2.0 ** 47, "mul", "max")
    tt(A("VA", 16, 16), A("VA", 0, 16), A("OH"), "mul")
    scan(A("VA", 32, 16), A("VA", 16, 16), A("OH"), 0.0, "max", "max")
    ts(A("THR"), A("DG"), col("VA", 47), "mul")
    ts(A("BOI"), A("BO32"), col("VA", 47), "mul", -0.5, "mul")
    ts(col("PF", 19), col("PF", 2), 16.0, "mul")
    iota(A("T2"), [[-16, 12], [4096, 16]], 191, -1)
    ts(A("TD"), A("T2"), col("PF", 19), "add")
    for b in range(2):
        iota(A("QW%d" % b, 0, 512), [[0, 512]], 0, 0)
    for b in ("UW", "C", "SD1", "SD2", "SD3"):
        iota(A(b, 0, 192), [[0, 192]], 0, 0)
    ts(A("XC", 0, 384, p=(0, 24)), A("IN", 0, 384, p=(0, 24)), A("PF", 17, 1, p=(0, 24)), "add")
    ts(A("XC", 384, 896, p=(0, 16)), A("IN", 384, 896, p=(0, 16)), A("PF", 17, 1, p=(0, 16)), "add")
    for lo, n in ((0, 512), (512, 512), (1024, 256)):
        ts(A("TF", lo, n), A("TL", lo, n), 0.0, "add")
    for k, (lo, n) in enumerate(((0, 384), (384, 512), (896, 384))):
        pa, pb = (("SA", "SB"), ("NA", "NB"), ("SA", "NC"))[k]
        mm(A(pa, 0, n), A("RR", 128, 128, p=(0, 8)), A("XC", lo, n, p=(0, 8)))
        act(A("SD0", 192 + lo, n), A(pa, 0, n), "Copy")
        mm(A(pb, 0, n), A("RR", 0, 128, p=(0, 16)), A("XC", lo, n, p=(0, 16)))
        tt(A("C", 192 + lo, n), A(pb, 0, n), A("SD0", 192 + lo, n), "mul")

    def send_sides(t):
        sd = "SD%d" % t
        mm(A("M0", 0, 192), A("IB"), A(sd, 192, 192))
        mm(A("M0", 192, 192), A("ROT"), A(sd, 384, 192))
        act(A("ST"), A("M0", 0, 384), "Copy")
        return send("as%d" % t, [(A(sd, 1472, 384), A("ST"))])

    def send_values(t):
        b, lo, so, land = ("UW", 192, "SO", 2240 + 384 * (t - 1)) if t else ("U0B", 0, "SOB", 2048)
        if cfg["one"]:
            mm(A("SL", 0, 192), A("I32" if t else "IB"), A(b, lo, 192))
            mm(A("SL", 192, 192), A("R32" if t else "ROT"), A(b, lo + 192, 192))
            act(A(so), A("SL", 0, 384), "Copy")
            send("ao%d" % t, [(A(b, land, 384), A(so))])
        else:
            mm(A("SL", 0, 192), A("R32" if t else "ROT"), A(b, lo + 192, 192))
            act(A(so, 0, 192), A("SL", 0, 192), "Copy")
            send("ao%d" % t, [(A(b, land, 192), A(b, lo, 192)), (A(b, land + 192, 192), A(so, 0, 192))])

    def view_lists(c0, c1):
        n = c1 - c0
        for b in range(16):
            mm(A("M1", 384 + c0, n), A("D32", 128 * b, 128), A("C", 192 + 16 * c0 + b, n, 16), b == 0, b == 15)
        cl = A("M1", 384 + c0, n)
        for z in (0, 1):
            v = A("VA", 80 * z + c0, n)
            tt(v, cl, A("ML", 80 * z + c0, n), ("max", "min")[z])
            ts(A("VL", 80 * z + c0, n), v, -1.0, ("add", "mul")[z])

    def views(t, c0, c1, split=False, after=None):
        for z in (0, 1):
            o, a = A("X%d" % t, 32 * c0 + z, 16 * (c1 - c0), 2), IND(A("UW", 192, 2048) if t else A("U0B", 0, 2048), A("VL", 80 * z + c0, c1 - c0))
            k = cp(o, a) if split and z else act(o, a, "Copy")
            if after is not None and ops[k]["e"] == ops[after]["e"]: ops[k]["after"] = after

    def send_views(t):
        x, sv = "X%d" % t, "SV" if t else "SVB"
        if t and cfg["rot"] == "Y":
            dma("Y", A(sv, p=(0, 112)), A(x, 384, 384, p=(16, 128)), 112, 1536)
            dma("Y", A(sv, p=(112, 128)), A(x, 384, 384, p=(0, 16)), 16, 1536)
        else:
            mm(A("SL", 0, 384), A("R32" if t else "ROT"), A(x, 384, 384))
            act(A(sv), A("SL", 0, 384), "Copy")
        return send("av%d" % t, [(A(x, 2560, 384), A(x, 0, 384)), (A(x, 2944, 384), A(sv))])

    def names(t):
        par, m = t % 2, max(2, t + 1)
        nm, sg = "NM%d" % par, "GH%d" % par
        ts(A(nm), IND(A("TL"), A("HU", 12 * par, 12)), 0.0, "add")
        ts(A(sg), A(nm), 1279.5, "gt")
        for hf in (0, 1):
            o = A("M1", 96 * hf, 96)
            for k in (0, 1):
                mm(o, A("PM", 128 * (2 * hf + k), 128), A(nm, k, 96, 2), k == 0, False)
            for k in range(2 * m):
                mm(o, A("PK", 128 * (2 * hf + k % 2), 128), A(sg, k % 2, 96, 2), False, k == 2 * m - 1)
        mm(A("M1", 192, 192), A("I16"), A(nm))
        cp(A("XL%d" % par), A("M1", 0, 384))

    send_values(0)
    send_sides(0)
    view_lists(0, 24)
    views(0, 0, 24, True)
    sent = send_views(0)
    ops[dma("G", A("UW", 1472, 768), ("w0", ALL), 128, 3072)]["behind"] = sent
    ops[dma("G", A("UW", 192, 1280), ("u0", ALL), 128, 5120)]["behind"] = sent
    def turn_names(blk, behind):
        w = (8, 8, 4)[blk]
        for gq in range(8):
            k = dma("Y", A("TS", 512 * blk + 64 * gq, 64, p=(0, 16 * w)), A("TF", 512 * blk, 64 * w, p=(16 * gq, 16 * gq + 16)), 16 * w, 128)
            ops[k]["behind"] = behind

    mm(A("M0", 0, 384), A("RR", 256, 128, p=(0, 24)), A("XC", 0, 384, p=(0, 24)))
    for par in (0, 1):
        tt(A("PR"), A("M0", par, 192, 2), A("DG"), "mul")
        scan(A("S1"), A("KEEP"), A("PR"), 0.0, "mul", "add")
        ts(A("HL", 12 * par, 12), A("S1", 15, 12, 16), 192.0, "add")
        cp(A("HU", 12 * par, 12), A("S1", 15, 12, 16))
    names(0)
    view_lists(24, 80)

    def ghost_views(t, after=None):
        view_lists(0, 80)
        views(t, 0, 24, "g" in cfg["vv"][t], after)
        send_views(t)

    def host_out(par):
        mm(A("SL", 0, 128, p=(0, 12)), A("HL", 12 * par, 12), A("I32"))
        act(A("YH", par, 128, 2, p=(0, 12)), A("SL", 0, 128, p=(0, 12)), "Identity", A("TH", 2, 1, p=(0, 12)))

    ms(col("TH", 2), -192.0)
    turn = {"bank": 0, "nd": 0, "xg": 0, "qn": 0}

    def take(kind, names):
        turn[kind] += 1
        return names[turn[kind] % len(names)]

    for t in range(RO):
        par, last, mark = t % 2, t == RO - 1, {}
        x, sd, nm, ti = "X%d" % t, "SD%d" % t, "NM%d" % par, "TI%d" % par
        if not last:
            dma("Y", A("SD%d" % (t + 1), 192, 1280), A(sd, 192, 1280), 128, 2560)
        if t:
            for j0, n in CHUNK.values():
                gcp(A("UR", 4 * j0, n), A("UW", 192 + t + 4 * j0, n, 4))
                gcp(A("UR", 4 * j0 + n, n), A("UR", 4 * j0, n))
                gcp(A("UR", 4 * j0 + 2 * n, 2 * n), A("UR", 4 * j0, 2 * n))
            for b in range(16):
                mm(A("NC", 320, 128, p=(0, 20)), A(sd, 192 + t + 4 * b, 20, 64), A("DB", 128 * b, 128), b == 0, b == 15)
            act(A("SLT", p=(0, 20)), A("NC", 320, 128, p=(0, 20)), "Copy")
            mm(A("NC", 0, 320), A("SLT", p=(0, 20)), A("REP", p=(0, 20)), True, False)
            for j0, k in CHUNK.values():
                mm(A("NC", j0, k), A("TS", 4 * j0 + t, 128, 4, p=(0, k)), A("I16", 0, k, p=(0, k)), False, k == 64)
            ts(A(ti), A("NC", 0, 320), 2.0, "mul", 0.5, "add")
        else:
            mm(A("NC", 0, 320), A("I16"), A("TF", 0, 320, 4), True, False)
            mm(A("NC", 0, 320), A("IQ"), A(sd, 192, 320, 4), False, True)
            ts(A(ti), A("NC", 0, 320), 2.0, "mul", 0.5, "add")
        for h in (2, 1, 0):
            m, el = "M%d" % (h % 2), A("EL", 64 * h, 64)
            eo, ei = A("EB", 1024 * h, 1024), IND(A(sd, 192, 1664), A("XL%d" % par, 192 + 64 * h, 64))
            if 2 - h in cfg["ev"][t]: cp(eo, ei)
            else: act(eo, ei, "Copy")
            for b in range(16):
                mm(A(m, 0, 64), A("DB", 128 * b, 128), A("EB", 1024 * h + b, 64, 16), b == 0, b == 15)
            act(el, A(m, 0, 64), "Relu")
            mm(A(m, 192, 64), A("IB"), A("KW", 64 * par, 64), True, False)
            for hf in (0, 1):
                for sg in (0, 1):
                    mm(A(m, 192 + 32 * hf, 32), A("PB", 128 * (2 * hf + sg), 128), A("EL", 64 * h + sg, 32, 2), False, hf + sg == 2)
            mm(A(m, 256, 64), A("IB"), A("KA", 0, 64), True, False)
            mm(A(m, 256, 64), A("IB"), A("KA", 64, 64), False, False)
            for li in (0, 1):
                for sg in (0, 1):
                    mm(A(m, 256 + 32 * li, 32), A("WA", 128 * (2 * li + sg), 128), A("EL", 64 * h + sg, 32, 2), False, li + sg == 2)
            cp(A("IX", 128 * h, 128), A(m, 192, 128))
            win = A("UW", 1472 + 256 * h, 256) if t else A("U0B", 1280 + 256 * h, 256)
            for c, n in (((0, 32), (32, 32)) if 2 - h in cfg["half"] else ((0, 64),)):
                mark["w%d" % (2 - h)] = act(A("WS%d" % h, 16 * c, 16 * n), IND(win, A("IX", 128 * h + c, n)), "Copy")
            for hf in (0, 1):
                own = IND(A("UW", 192, 2048 + 384 * t) if t else A("U0B"), A("XL%d" % par, 96 * hf + 32 * h, 32))
                tt(A("D%d" % h, 512 * hf, 512), own, A("WS%d" % h, 512 * hf, 512), "sub")
        if not t:
            for blk in range(3): turn_names(blk, mark["w0"])
        if t and cfg["vg"] != "early": ghost_views(t, mark.get(cfg["vg"]))
        if not last: names(t + 1)
        ghost = A("GH%d" % par)
        mm(A("M0", 0, 192), A("IB"), A("EL"), True, False)
        mm(A("M0", 0, 192), A("IN1"), ghost, False, True)
        mm(A("M0", 192, 192), A("IN1"), A("EL"), True, False)
        mm(A("M0", 192, 192), A("IN1"), ghost, False, True)
        act(A("FIT", 0, 192), A("M0", 0, 192), "Relu")
        act(A("FIT", 192, 192), A("M0", 192, 192), "Relu", 1.0)
        for z in (0, 1):
            mm(A("M0", 192 * z, 192), A("MT"), A("FIT", 192 * z, 192), True, False)
            mm(A("M0", 192 * z, 192), A("I16"), A(nm), False, True)
        act(A("VAL"), A("M0", 0, 384), "Relu", 192.0 - 2048.0)
        mm(A("M0", 0, 384), A("BO32"), A("VAL"))
        act(A("CAND"), A("M0", 0, 384), "Copy")

        def summ(o, terms):
            for k, a in enumerate(terms):
                mm(o, A("I32"), a, k == 0, k == len(terms) - 1)

        def shock(k):
            h = 2 - k
            d, q, bb, how = "D%d" % h, "QW%d" % (h % 2), "WS%d" % h, cfg["pair"][k]
            lo, hi, o, pa, pb = A(q, 512, 512), A(q, 1024, 512), A(q, 1536, 512), A("SA"), A("SB")
            act(pa, A(d, 0, 512), "Abs")
            tt(lo, A(d, 0, 512), pa, "mul")
            act(pb, A(d, 512, 512), "Abs")
            tt(pb if how == "s" else hi, A(d, 512, 512), pb, "mul")
            if how == "s":
                tt(o, lo, pb, "add")
                act(hi, pb, "Copy")
            elif how == "t":
                summ(pa, [lo, hi])
                act(o, pa, "Copy")
            else:
                tt(o, lo, hi, "add")
            mark["g%d" % k] = act(A(bb, 512, 512), IND(A(q), A("IX", 128 * h + 96, 32)), "Copy")
            tt(A(bb, 0, 512), IND(A(q), A("IX", 128 * h + 64, 32)), A(bb, 512, 512), "add")
            r = A("SL", 128 * h, 128)
            if k in cfg["c1"]:
                summ(A("SL", 384, 128), [A(bb, 1, 128, 4), A(bb, 3, 128, 4)])
                act(A(d, 0, 128), A("SL", 384, 128), "Copy")
            else:
                tt(A(d, 0, 128), A(bb, 1, 128, 4), A(bb, 3, 128, 4), "add")
            summ(r, [A(bb, 0, 128, 4), A(bb, 2, 128, 4), A(d, 0, 128)])
            act(r, r, "Copy", 0.0, 2.0 ** -6)
            for z in (0, 1):
                tt(A("WN", 192 * z + 64 * h, 64), A("UW", 1472 + 256 * h + 2 * par + z, 64, 4), A("SL", 128 * h + z, 64, 2), "add")

        def node(ch):
            j0, n = CHUNK[ch]
            q, c = take("qn", ("QN0", "QN1")), cfg["cb"] if ch == "c" else "NC"
            u = A("UR", 4 * j0, 4 * n)
            if not t:
                for lo in range(0, n, 64):
                    (cp if ch + str(lo // 64) in cfg["pe"][0] else lambda o, a: act(o, a, "Copy"))(A("XB", 16 * lo, 1024), IND(A(x), A(ti, j0 + lo, 64)))
            for k in (0, 2, 1, 3):
                p = A(take("bank", ("NA", "NB") if ch == "a" else ("NA", "NB", "SA", "SB")), 0, 4 * n)
                d = A(take("nd", ("ND0", "ND1", "ND2")), 0, 4 * n)
                xs = IND(A(x), A(ti, j0 + k * n // 4, n // 4))
                if not t:
                    for m in range(4):
                        mm(A(p["b"], m * n, n), A("IB"), A("XB", 4 * k + m, n, 16), True, False)
                        mm(A(p["b"], m * n, n), A("IN1"), A("U0B", 4 * j0, n, 4), False, True)
                    act(d, p, "Abs")
                elif "%s%d" % (ch, k) in cfg["pe"][t]:
                    xg = A(take("xg", ("XG0", "XG1")), 0, 4 * n)
                    act(xg, xs, "Copy")
                    mm(p, A("I32"), xg, True, False)
                    mm(p, A("N32"), u, False, True)
                    act(d, p, "Abs")
                else:
                    tt(d, xs, u, "sub")
                    act(p, d, "Abs")
                if k == 2:
                    tt(p, d, p, "mul")
                    tt(A(q, 0, 4 * n), A(q, 0, 4 * n), p, "add")
                elif k == 3 and ch in cfg["tree"][t]:
                    c3 = p["b"]
                    tt(A(c3, 0, 3 * n), A(d["b"], 0, 3 * n), A(c3, 0, 3 * n), "mul")
                    tt(A(q, 11 * n, n), A(d["b"], 3 * n, n), A(c3, 3 * n, n), "mul")
                else:
                    tt(A(q, 4 * n * min(k, 2), 4 * n), d, p, "mul")
            if ch in cfg["tree"][t]:
                tt(A(c3, 0, 3 * n), A(c3, 0, 3 * n), A(q, 4 * n, 3 * n), "add")
                tt(A(c3, 2 * n, n), A(c3, 2 * n, n), A(q, 2 * n, n), "add")
            else:
                c3 = c
                mm(A(c, 0, 3 * n), A("I32"), A(q, 4 * n, 3 * n), True, False)
                mm(A(c, 0, 3 * n), A("I32"), A(q, 8 * n, 3 * n), False, False)
                mm(A(c, 2 * n, n), A("I32"), A(q, 2 * n, n), False, True)
            tt(A(q, 0, 2 * n), A(q, 0, 2 * n), A(c3, 0, 2 * n), "add")
            tt(A(q, 0, n), A(q, 0, n), A(c3, 2 * n, n), "add")
            r = A(c, 3 * n, n)
            summ(r, [A(q, 7 * n, n), A(q, 11 * n, n), A(q, 3 * n, n), A(q, n, n), A(q, 0, n)])
            un = A("UW", 192 + t + 4 * j0, n, 4)
            if ch == "a": act(r, r, "Copy", 0.0, 2.0 ** -6)
            else: tt(r, r, A("MK", j0 - 128, n), "mul")
            tt(un, un, r, "add")

        def claims(lo, n):
            w0, w1 = A("WN", lo, n), A("WN", 192 + lo, n)
            if cfg["dd"] == "T":
                dd = A("M1", 384, n)
                mm(dd, A("I32"), w0, True, False)
                mm(dd, A("N32"), w1, False, True)
            else:
                dd = A("DD", lo, n)
                tt(dd, w0, w1, "sub")
            ts(A("CMP", lo, n), dd, col("TH", 4), "gt", 0.59375, "sub")
            ts(A("CMP", 192 + lo, n), dd, col("TH", 1), "lt", 0.59375, "sub")
            for z in (0, 1):
                mm(A("M1", 192 * z + lo, n), A("BOK"), A("CMP", 192 * z + lo, n))
            tt(A("MM", lo, n), A("M1", lo, n), A("CAND", lo, n), "min")
            tt(A("M1", 384, n), A("M1", 192 + lo, n), A("CAND", 192 + lo, n), "min")
            tt(A("VV", lo, n), A("MM", lo, n), A("M1", 384, n), "max")
            tt(A("PR", lo, n), A("VV", lo, n), A("DG", lo, n), "mul")
            scan(A("S1", lo, n), A("KEEP", lo, n), A("PR", lo, n), 0.0, "mul", "add")
            for c in range(lo // 16, (lo + n) // 16):
                k, o = 192 - 16 * c, 8 * c * (25 - c)
                ts(A("EQ", o, k), A("VV", 16 * c, k), col("S1", 16 * c + 15), "eq")
                if k > 16: mm(A("M0", 16 * c + 16, k - 16), A("BOB"), A("EQ", o + 16, k - 16), False, False)
                mm(A("M0", 16 * c, 16), A("BOI"), A("EQ", o, 16), False, lo == 0 and 16 * c + 16 == n)

        mm(A("M0", 0, 192), A("IB"), A("THR"), True, False)
        for k in range(3):
            shock(k)
            if k == 0 and cfg["cl"] == 3: claims(128, 64)
            if k == 1: claims(*((64, 64) if cfg["cl"] == 3 else (64, 128)))
        claims(0, 64)
        for c0, c1 in cfg["vr"]: views(t, c0, c1, "r" in cfg["vv"][t], mark.get(cfg["vra"]))
        node("a")
        for z in (0, 1):
            gcp(A("UW", 1472 + 2 * par + z, 192, 4), A("WN", 192 * z, 192))
        if last: dma("Y", ("ys", ALL), A("UW", 1472, 768), 128, 3072)
        tt(A("MW"), A("M1", 0, 384), A("WN"), "min")
        act(A("DN"), A("M1", 192, 192), "Sign")
        tt(A("PR"), A("M0", 0, 192), A("VV"), "min")
        scan(A("S2"), A("TD"), A("PR"), 1e6, "min", "max")
        pos, pu = A("S2", 15, 12, 16), A("PU")
        cp(pu, pos)
        if not last:
            cp(IND(A("SD%d" % (t + 1), 0, 1472), pu), A("DN"))
            send_sides(t + 1)
        tt(IND(A("C"), pu), A("DN"), A("W2S", par, 192, 2), "mul")
        hl, ha = A("HL", 12 * par, 12), A("HA", 0, 12)
        ts(ha, pos, 192.0, "lt", 4096.0, "mul")
        tt(ha, ha, hl, "min")
        tt(hl, ha, pos, "max")
        if t < 2:
            ts(A("HU", 12 * par, 12), hl, -192.0, "add")
        else:
            host_out(par)
        if last:
            for b in range(16):
                mm(A("M1", 384, 80), A("D32", 128 * b, 128), A("C", 192 + 80 * b, 80), b == 0, b == 15)
            ts(A("VA", 0, 80), A("M1", 384, 80), -1280.0, "add")
            ts(A("VA", 80, 80), A("M1", 384, 80), -1.0, "mul", -1281.0, "add")
            tt(A("VA", 0, 80), A("VA", 0, 80), A("VA", 80, 80), "max")
            dma("Y", ("yc", ALL), A("VA", 0, 80), 128, 320)
            for gq in range(8):
                dma("Y", ("yh", (gq, slice(None))), A("YH", 32 * gq, 32, p=(0, 12)), 12, 128)
        tt(IND(A("UW", 0, 1472), pu), A("MW", 0, 192), A("MW", 192, 192), "max")
        if not last:
            send_values(t + 1)
            if cfg["vg"] == "early": ghost_views(t + 1)
            new = A("SD%d" % (t + 1), 192 + t + 512, 192, 4)
        else:
            dma("Y", ("yu", (slice(None), slice(0, 512))), A("UW", 192, 512), 128, 2048)
            new = A("SN")
            act(new, A("C", 192 + t + 512, 192, 4), "Sign")
        mm(A("M0", 0, 192), A("IB"), new, True, False)
        mm(A("M0", 0, 192), A("IB"), A(sd, 192 + t + 512, 192, 4), False, True)
        act(A("MK"), A("M0", 0, 192), "Abs", 0.0, 2.0 ** -7)
        for ch in "bc":
            node(ch)
            j0, n = CHUNK[ch]
            if last: dma("Y", ("yu", (slice(None), slice(4 * j0, 4 * (j0 + n)))), A("UW", 192 + 4 * j0, 4 * n), 128, 16 * n)
    return ops


ASYNC = ("dma", "rem", "arr")
HOP, ROW, RATE = 0.1, 0.08, 2e4


def plan(cfg):
    ops = build_ops(cfg)
    hist = {}
    for i, o in enumerate(ops):
        dep = {}
        for acc, w in ((o["rd"], False), (o["wr"], True)):
            for s in acc:
                b, lo, hi = s[:3]
                for s2, j, w2 in hist.get(b, ()):
                    if b in PS and ops[j]["e"] != o["e"]:
                        if lo // 512 <= (s2[2] - 1) // 512 and s2[1] // 512 <= (hi - 1) // 512: dep[j] = True
                    elif (w or w2) and o["k"] != "arr" and meet(s, s2):
                        dep[j] = dep.get(j, False) or not (b in PS and o.get("acc"))
        if o["k"] == "mm":
            b, lo = o["wr"][0][:2]
            for s2, j, w2 in hist.get(b, ()):
                if w2 and ops[j]["k"] == "mm" and s2[1] // 512 == lo // 512 and j not in dep: dep[j] = False
        if "after" in o: dep.setdefault(o["after"], False)
        if "behind" in o: dep[o["behind"]] = True
        o["dep"] = dep
        for acc, w in ((o["rd"], False), (o["wr"], True)):
            for s in acc:
                h = hist.setdefault(s[0], [])
                if w and s[3] == 1 and s[4] == (0, 128) and o["k"] != "arr" and not o.get("acc"):
                    h[:] = [r for r in h if not (s[1] <= r[0][1] and r[0][2] <= s[2] and dep.get(r[1]))]
                h.append((s, i, w))
    n = len(ops)
    pred, succ = [[] for _ in range(n)], [[] for _ in range(n)]
    anc = [0] * n
    for i, o in enumerate(ops):
        for j in o["dep"]: anc[i] |= anc[j]
        far = anc[i]
        for j, hard in o["dep"].items():
            anc[i] |= 1 << j
            if far >> j & 1 and not ops[j]["lat"]: continue
            d = ops[j]["lat"] + HOP if (hard or o["k"] == "arr") else 0.0
            pred[i].append((j, d))
            succ[j].append((i, d))
    cost, eng = [o["cost"] + 1e-6 for o in ops], [o["e"] for o in ops]

    rnd = [cfg["seed"]]

    def draw():
        rnd[0] = (rnd[0] * 1103515245 + 12345) % 2147483648
        return (rnd[0] + 0.5) / 2147483648

    def place(seq, before, rel, free):
        st, busy = {}, {e: [(-1.0, free[e])] for e in free}
        for i in seq:
            s, c = rel[i], cost[i]
            for j, d in before[i]:
                x = st[j] + d
                if x > s: s = x
            b = busy[eng[i]]
            lo = len(b)
            if b[-1][1] > s:
                lo, hi = 0, lo - 1
                while lo < hi:
                    m = (lo + hi) // 2
                    if b[m][1] <= s: lo = m + 1
                    else: hi = m
                while lo < len(b) and b[lo][0] < s + c:
                    s = b[lo][1]
                    lo += 1
            b.insert(lo, (s, s + c))
            st[i] = s
        return st, busy

    def improve(calls, key, head, tail, free, after, steps, heat):
        mine = set(calls)
        pre = {i: [(j, cost[j] + d) for j, d in pred[i] if j in mine] for i in calls}
        suc = {i: [(j, cost[j] + d) for j, d in succ[i] if j in mine] for i in calls}

        def span_of(st, busy):
            i = max(calls, key=lambda i: st[i] + cost[i] + tail[i])
            end = st[i] + cost[i] + tail[i]
            for e, b in busy.items():
                if len(b) > 1 and b[-1][1] + after[e] > end: end, i = b[-1][1] + after[e], e
            return end, st, i

        def both(st):
            back = place(sorted(calls, key=lambda i: -st[i] - cost[i]), suc, tail, after)[0]
            return place(sorted(calls, key=lambda i: -back[i] - cost[i]), pre, head, free)

        now = best = span_of(*place(sorted(calls, key=lambda i: key[i]), pre, head, free))
        pairs = None
        for it in range(steps):
            if pairs is None:
                iss, prev, lastq, pairs = now[1], {}, {}, []
                for i in sorted(calls, key=lambda i: iss[i]):
                    prev[i] = lastq.get(eng[i])
                    lastq[eng[i]] = i
                i = lastq.get(now[2], now[2])
                while i is not None:
                    s, k = head[i], None
                    for j, d in pre[i]:
                        if iss[j] + d > s: s, k = iss[j] + d, j
                    if s < iss[i] - 1e-7:
                        k = prev[i]
                        if k is not None: pairs.append((k, i))
                    i = k
            if not pairs: break
            key = dict(now[1])
            p, i = pairs[int(draw() * len(pairs))]
            if draw() < 0.5:
                while draw() < 0.5 and prev[p] is not None: p = prev[p]
                key[i] = key[p] - 1e-4
                todo = [i]
                while todo:
                    k = todo.pop()
                    for j, d in pre[k]:
                        if key[j] >= key[k]:
                            key[j] = key[k] - 1e-7
                            todo.append(j)
            else:
                key[p] = key[i] + 1e-4 + (draw() < 0.3) * 2 * draw()
                todo = [p]
                while todo:
                    k = todo.pop()
                    for j, d in suc[k]:
                        if key[j] <= key[k]:
                            key[j] = key[k] + 1e-7
                            todo.append(j)
            got = place(sorted(calls, key=lambda i: key[i]), pre, head, free)
            got = span_of(*(both(got[0]) if it % cfg["fbe"] == 0 else got))
            if got[0] <= now[0] - heat * (1 - it / steps) * math.log(draw()): now, pairs = got, None
            if got[0] < best[0]: best = got
        return best

    zero, lats, idle, every = [0.0] * n, [o["lat"] for o in ops], {e: 0.0 for e in "VSTGYR"}, list(range(n))
    top = [0.0] * n
    for i in range(n - 1, -1, -1):
        top[i] = cost[i] + max([lats[i]] + [top[k] + d + 1e-9 for k, d in succ[i]])
    best = improve(every, [-x for x in top], zero, lats, idle, idle, cfg["all"], cfg["heat"])
    allsuc = {i: [(j, cost[j] + d) for j, d in succ[i]] for i in every}
    t0 = 0.0
    for it in range(cfg["ls"]):
        iss, t1 = best[1], t0 + cfg["wide"]
        back = place(sorted(every, key=lambda i: -iss[i] - cost[i]), allsuc, lats, idle)[0]
        calls = [i for i in every if t0 <= iss[i] < t1]
        head, tail, free, after = {}, {}, dict(idle), dict(idle)
        for i in every:
            if iss[i] < t0: free[eng[i]] = max(free[eng[i]], iss[i] + cost[i])
            elif iss[i] >= t1: after[eng[i]] = max(after[eng[i]], back[i] + cost[i])
        for i in calls:
            head[i] = max([0.0] + [iss[j] + cost[j] + d for j, d in pred[i] if iss[j] < t0])
            tail[i] = max([lats[i]] + [back[j] + cost[j] + d for j, d in succ[i] if iss[j] >= t1])
        st = improve(calls, iss, head, tail, free, after, cfg["steps"], cfg["heat"])[1]
        key = [st[i] if i in st else iss[i] if iss[i] < t0 else 1e4 - back[i] - cost[i] for i in every]
        got = improve(every, key, zero, lats, idle, idle, 0, 0)
        if got[0] <= best[0] + cfg["slack"]: best = got
        t0 = t0 + cfg["wide"] * (0.2 + 0.3 * draw()) if t1 < best[0] else 0.0
    iss = best[1]
    fin = [iss[i] + cost[i] + lats[i] for i in range(n)]
    order = sorted(range(n), key=lambda i: iss[i])
    ready = "VSTGYR"
    cnt = {e: 0 for e in ready}
    know = {e: {} for e in ready}
    nd = 0
    for i in order:
        o = ops[i]
        kn = know[o["e"]]
        waits = {}
        for j, hard in o["dep"].items():
            if hard and kn.get(ops[j]["id"][0], 0) < ops[j]["id"][1]:
                s, v = ops[j]["id"]
                if v > waits.get(s, (0, 0))[0]: waits[s] = (v, j)
        todo = sorted(waits.items(), key=lambda w: -fin[w[1][1]])
        o["waits"] = []
        for s, (v, j) in todo:
            if kn.get(s, 0) >= v: continue
            o["waits"].append((s, v))
            kn[s] = v
            for s2, v2 in ops[j]["clock"].items():
                if kn.get(s2, 0) < v2: kn[s2] = v2
        if o["k"] == "arr":
            o["id"], o["clock"] = (o["sem"], 1), {}
        elif o["k"] in ASYNC:
            o["id"], o["clock"] = ("d%d" % nd, 1), dict(kn)
            nd += 1
        else:
            cnt[o["e"]] += len(o["a"]) if o["k"] == "mm" else 1
            o["id"], o["clock"] = ("c" + o["e"], cnt[o["e"]]), dict(kn)
    return ops, order, cnt, nd, iss, fin


OPS, ORDER, CNT, NDMA, ISS, FIN = plan(CFG)
SEMAPHORES = ["cV", "cS", "cT", "cG"] + ["d%d" % k for k in range(NDMA)] + [k + str(t) for k in ("as", "ao", "av") for t in range(RO)]
ALU = {"add": AluOpType.add, "sub": AluOpType.subtract, "mul": AluOpType.mult, "max": AluOpType.max, "min": AluOpType.min,
       "ge": AluOpType.is_ge, "gt": AluOpType.is_gt, "lt": AluOpType.is_lt, "eq": AluOpType.is_equal,
       "and": AluOpType.bitwise_and, "shr": AluOpType.arith_shift_right}
FUN = {"Copy": ActivationFunctionType.Copy, "Identity": ActivationFunctionType.Identity, "Abs": ActivationFunctionType.Abs,
       "Sign": ActivationFunctionType.Sign, "Relu": ActivationFunctionType.Relu}


def rank_program(g, core, T, topo):
    rank = T.rank_of(core)
    if rank is None:
        return
    n = len(T.cores)
    dst, src = T.cores[(rank - 1) % n], T.cores[(rank + 1) % n]
    rid, pid, _ = topo.addr(dst)
    eout, ein = topo.engines(core, dst), topo.engines(src, core)
    Q = {"V": g.vector, "S": g.scalar, "T": g.tensor, "G": g, "Y": g.sync}

    def ap(a):
        if isinstance(a, tuple): return T[a[0]][a[1]]
        if not isap(a): return a
        if "off" in a:
            return T[a["b"]][:, a["lo"]:a["lo"] + a["wn"]].indirect(ap(a["off"]))
        cs = slice(a["lo"], a["lo"] + (a["n"] - 1) * a["st"] + 1, a["st"]) if a["st"] > 1 else slice(a["lo"], a["lo"] + a["n"])
        return T[a["b"]][slice(*a["p"]), cs]

    full = {}
    for o in OPS:
        if o["k"] == "arr": full[o["id"][0]] = len(ein) // o["ntr"] * o["ntr"]
        elif o["k"] == "rem": full[o["id"][0]] = len(eout) // len(o["tr"]) * len(o["tr"])
        elif o["k"] == "dma": full[o["id"][0]] = 16
    for i in ORDER:
        o = OPS[i]
        k = o["k"]
        if k == "arr": continue
        q = Q[o["e"]]
        for s, v in o["waits"]:
            q.wait_ge(T.sem[s], v * full.get(s, 1))
        sem = T.sem[o["id"][0]]
        if k == "rem":
            per = len(eout) // len(o["tr"])
            if len(o["tr"]) == 1:
                g.remote_dma(ap(o["tr"][0][0]), ap(o["tr"][0][1]), T.sem[o["sem"]], sem, pid, rid, topo.mask(core, dst))
            else:
                g.remote_dma_fused([RemoteDMATransfer(dst_ids=[DstId(rid=rid, pnc=pid)], dma_engine_mask=sum(1 << e for e in eout[m * per:(m + 1) * per]),
                                                      remote_sem=T.sem[o["sem"]], src=ap(b), dst=ap(a)) for m, (a, b) in enumerate(o["tr"])], local_sem=sem)
            continue
        a = o["a"]
        if k == "dma":
            q.dma_start(ap(a[0]), ap(a[1])).then_inc(sem, 16)
            continue
        if k == "mm":
            for m in a: q.matmul(ap(m[0]), ap(m[1]), ap(m[2]), m[3], m[4]).then_inc(sem, 1)
            continue
        if k == "tt": r = q.tensor_tensor(ap(a[0]), ap(a[1]), ap(a[2]), ALU[a[3]])
        elif k == "ts":
            if a[5] is None: r = q.tensor_scalar(ap(a[0]), ap(a[1]), ap(a[2]), None, ALU[a[4]])
            else: r = q.tensor_scalar(ap(a[0]), ap(a[1]), ap(a[2]), ap(a[3]), ALU[a[4]], ALU[a[5]])
        elif k == "cp": r = q.tensor_copy(ap(a[0]), ap(a[1]))
        elif k == "gcp": r = q.affine_select(ap(a[0]), ap(a[1]), [[1, a[0]["n"]]], ALU["ge"], 0.0, 0, 0)
        elif k == "ms": r = q.memset(ap(a[0]), a[1])
        elif k == "scan": r = q.tensor_tensor_scan(ap(a[0]), ap(a[1]), ap(a[2]), a[3], ALU[a[4]], ALU[a[5]])
        elif k == "act": r = q.activation(ap(a[0]), ap(a[1]), FUN[a[2]], bias=ap(a[3]), scale=ap(a[4]))
        elif BUF[a[0]["b"]][1] == I: r = q.iota(ap(a[0]), a[1], a[2], a[3])
        else: r = q.iota(ap(a[0]), a[1], a[2], a[3], allow_small_or_imprecise_dtypes=True)
        r.then_inc(sem, 1)
    for e in "VSTG":
        g.wait_ge(T.sem["c" + e], CNT[e])
    for s, v in full.items():
        g.wait_ge(T.sem[s], v)
